import numpy as np, ml_dtypes
CORES = [66,74,82,90,194,202,210,218]
N = 8
import mx_ref
BF = ml_dtypes.bfloat16
def gcols(t, e):
    v = np.concatenate([t.reshape(8, 16, -1, 4), np.zeros((8, 16, 1, 4), BF)], axis=2)
    return np.ascontiguousarray(np.stack([v[g][:, e[g]] for g in range(8)])).reshape(128, -1)
def tile(rs):
    return np.stack(rs, axis=2).reshape(128, -1).astype(BF)
def pick(q, e):
    c = np.concatenate([q[0].reshape(128, -1, 4), np.zeros((128, 1, 4), np.uint8)], axis=1); s = np.concatenate([q[1], np.ones((16, 1), np.uint8)], axis=1)
    return (np.ascontiguousarray(c[:, e].reshape(128, -1)), np.ascontiguousarray(s[:, e]))
def join(*qs):
    return (np.concatenate([q[0] for q in qs], axis=1), np.concatenate([q[1] for q in qs], axis=1))
def put(q, e, v):
    c, s = q[0].reshape(128, -1, 4).copy(), q[1].copy(); c[:, e] = v[0].reshape(128, -1, 4); s[:, e] = v[1]
    return (c.reshape(128, -1), s)
def pk(c, s):
    return (np.ascontiguousarray(c), mx_ref.live(s))
def emit(q):
    return q[0], q[1]
def packed(v, rng):
    q = [mx_ref.quantize(np.ascontiguousarray(v[r])) for r in range(N)]
    return np.stack([a for a, b in q]), np.stack([mx_ref.plane(b, rng) for a, b in q])
def values_of_codes():
    e, c = np.zeros((128, 128, 4), np.float32), np.zeros((128, 2, 4), np.uint8)
    e[np.arange(128), np.arange(128), 0] = 1
    c[:127, :, 0] = np.arange(256).reshape(2, 128).T[:127]
    return mx_ref.matmul(mx_ref.quantize(e.reshape(128, 512).astype(BF)), (c.reshape(128, 8), np.full((16, 2), 127, np.uint8))).T.reshape(-1).astype(np.float64)
CODE_VALUE, SCALE_VALUE = values_of_codes(), 2.0 ** (np.arange(256) - 127.0)
def decode(q):
    return (CODE_VALUE[q[0]].reshape(16, 8, -1, 4) * SCALE_VALUE[q[1]][:, None, :, None] + 0.0).reshape(128, -1).astype(np.float32)
def f(rng, *shape):
    return mx_ref.flush((rng.standard_normal(shape, dtype=np.float32) * np.exp2(rng.integers(-2, 3, shape[:-1] + (1,)))).astype(BF))
def wide(rng, *shape, cols=0):
    v = rng.standard_normal(shape, dtype=np.float32) * np.exp2(rng.integers(-12, 13, shape)).astype(np.float32)
    if cols: v *= np.repeat(np.exp2(rng.integers(-cols, cols + 1, shape[:-2] + (1, shape[-1] // 4))) * (rng.random(shape[:-2] + (1, shape[-1] // 4)) > 0.0625), 4, axis=-1).astype(np.float32)
    return mx_ref.flush(v.astype(BF))
C, S = 384, 48
def order(p):
    return np.argsort(-(p[::16] + np.float32(0.0)), axis=1, kind="stable")
def places(o):
    return np.argsort(o, axis=1)
def numbers_of(rng):
    return {"x": np.array(f(rng, N, 128, 4 * C)), "u": np.array(f(rng, N, 128, 512)), "v": np.array(f(rng, N, 128, 512)), "m": np.array(f(rng, N, 128, 512))}
def weights(rng, w):
    c, p = packed(w, rng)
    return {"wc": c, "ws": p}
def unit(rng, a, b, low=False):
    w = np.zeros((N, 128, 4, 128, 4), np.float32)
    i = np.arange(128)
    j = i[i % 16 // 4 == 2]
    for k in range(4):
        w[:, i, k, i, k] = np.where(i % 16 < 8, a, b)
        if low: w[:, j + 4, k, j, k] = b
    return weights(rng, w.reshape(N, 128, 2048).astype(BF))
def signs(rng):
    return np.stack([rng.permutation(8) % 2 * 2.0 - 1.0 for r in range(N)])
def digits(s):
    return np.stack([s // 64 * 64, s // 8 % 8 * 8, s % 8, 0 * s], axis=-1)
def setup_inputs(rng):
    return {**numbers_of(rng), **weights(rng, f(rng, N, 128, 2048))}
def setup_inputs_ties(rng):
    d = numbers_of(rng)
    e = rng.permutation(N)
    x = d["x"].reshape(N, 8, 16, C, 4)
    for r in range(N):
        k = np.zeros(C, int) if r == e[0] else rng.permutation(C) % 3
        a = np.abs(x[r][:, :8, :3].astype(np.float32))
        a[:, :, 2] = 0
        x[r][:, :8] = a[:, :, k].astype(BF)
        if r == e[2]:
            z = np.flatnonzero(k == 2)
            n = int(rng.integers(0, len(z) - 15))
            x[r][:, :, z[n:n + 16]] = 0
    x[e[1]][:, :8] = x[e[0]][:, :8]
    u, v = d["u"].reshape(N, 8, 16, 128, 4), d["v"].reshape(N, 8, 16, 128, 4)
    u[:, :, 8:, ::16] = 0
    v[:, :, 8:, ::16] = 0
    w = np.array(f(rng, N, 128, 2048)).astype(np.float32).reshape(N, 8, 16, 4, 8, 16, 4)
    w[:, :, 8:, :, :, :8] = 0
    w[:, :, :8, :, :, 8:] = 0
    w[:, :, :8, :, :, :8] = 0.0 - np.abs(w[:, :, :8, :, :, :8])
    return {"x": x.reshape(N, 128, 4 * C), "u": u.reshape(N, 128, 512), "v": v.reshape(N, 128, 512), "m": d["m"], **weights(rng, w.reshape(N, 128, 2048).astype(BF))}
def setup_inputs_near(rng):
    d = numbers_of(rng)
    x = d["x"].astype(np.float32).reshape(N, 8, 16, C, 4)
    s = (np.arange(C) // 2 + rng.integers(0, C // 2, (N, 8, 1))) % (C // 2)
    g = ((s[..., None] >> np.arange(8)) & 1) * np.exp2(np.arange(8) - 23.0)
    x[:, :, 0] = 0
    x[:, :, 0, :, 0] = -1
    x[:, :, 8] = 0.0 - g[..., :4]
    x[:, :, 9] = 0.0 - g[..., 4:]
    x[:, :, 10:] = rng.integers(4, 8, (N, 8, 6, C, 4)) * rng.choice([-1.0, 1.0], (N, 8, 6, C, 4)) * 2.0 ** -20
    x = x * np.float32(2.0 ** 16)
    u, v = d["u"].reshape(N, 128, 128, 4), d["v"].reshape(N, 128, 128, 4)
    u[:, :, ::16] = 0
    v[:, :, ::16] = 0
    a, b = (signs(rng) * -2.0 ** -30).astype(np.float32).astype(BF), (signs(rng) * -2.0 ** -30).astype(np.float32).astype(BF)
    for h in range(0, 128, 16):
        u[:, h, h, 0] = a[:, h // 16]
        v[:, h, h, 0] = b[:, h // 16]
        u[:, h + 8:h + 10, h] = -2.0 ** -30
        v[:, h + 8:h + 10, h] = 2.0 ** -30
    return {"x": x.reshape(N, 128, 4 * C).astype(BF), "u": u.reshape(N, 128, 512), "v": v.reshape(N, 128, 512), "m": d["m"], **unit(rng, 256, 256)}
def setup_inputs_huge(rng):
    d = numbers_of(rng)
    x = np.zeros((N, 8, 16, C, 4))
    e = rng.permutation(N)
    one = rng.permutation(N) < N // 2
    both = rng.permutation(N // 2) % 2
    for r in range(N):
        s = np.ones(N) if one[r] else rng.permutation(N) % 2 * 2.0 - 1.0
        val = np.sort(np.r_[0.875, 1 + 0.125 * np.arange(N - 1)] * 2.0 ** 29 * s)[::-1]
        lev = rng.permutation(C) % N
        x[r][:, :8] = val[lev][:, None]
        x[r][:, 8:] = 2.0 ** 13 * (0.5 + 0.5 * rng.random((8, 8, C, 4)))
        h = np.sort(rng.permutation(S)[:2])
        for l in range(N):
            j = np.flatnonzero(lev == l)[h]
            k = both[min(l, N - 1 - l)]
            if r == e[0]: x[r][:, 8:, j] = np.array([1.75, 1.625] if k else [1.625, 1.75])[:, None] * 2.0 ** 24
            if r == e[1] and k: x[r][:, 8:, j[0]] = -1.625 * 2.0 ** 24
    u, v = d["u"].reshape(N, 8, 16, 128, 4), d["v"].reshape(N, 8, 16, 128, 4)
    for t, p in ((u, slice(0, 8)), (v, slice(8, 16))):
        a = 2.0 ** 30 * (1 - 0.125 * rng.random((N, 8, 8, 8, 4))) * signs(rng)[:, None, None, :, None]
        t[:, :, :, ::16] = 0
        t[:, :, p, ::16] = a.astype(np.float32).astype(BF)
    return {"x": x.astype(np.float32).reshape(N, 128, 4 * C).astype(BF), "u": u.reshape(N, 128, 512), "v": v.reshape(N, 128, 512), "m": d["m"], **unit(rng, 0.015625, 4096)}
def setup_inputs_scan(rng):
    d = numbers_of(rng)
    i = np.arange(C)
    a = rng.integers(1, 26, (N, 8, 1))
    at = a + 26 * rng.integers(0, (C - 93) // 26 + 1, (N, 8, 1))
    two = np.stack([rng.permutation(8) < 2 for r in range(N)])[..., None]
    far = two & (i >= at) & (i < at + 68)
    n = np.where(two & (i >= at + 68), i - at - 68, i - a)
    since = np.where(far, i - at, np.where(i < a, i, n % 26))
    anew = far & (since == 40)
    quiet = (i >= a) & (n // 26 % 2 == 1)
    shape = (N, 8, C, 4, 4)
    kind = rng.choice(5, shape, p=[0.2, 0.1, 0.2, 0.35, 0.15])
    kind = np.where(quiet[..., None, None] & (kind < 3), 3, kind)
    kind = np.where(far[..., None, None], 4, kind)
    kind = np.where((since == 0)[..., None, None], 5, kind)
    kind[..., 3] = np.where(anew[..., None], 5, kind[..., 3])
    top = 16 * rng.integers(8, 13, shape) + rng.integers(7, 10, shape)
    rest = rng.integers(128, 240, shape)
    h, now = np.zeros(shape, int), np.zeros((N, 8, 4, 4), int)
    for k in range(C):
        t = kind[:, :, k]
        now = np.where(t == 5, top[:, :, k], now)
        h[:, :, k] = np.select([t == 0, t == 1, t == 2, t == 3, t == 5], [now - 1, now + 1, rest[:, :, k], -rest[:, :, k], now], 0)
        now = now + (t == 1)
    head = far & (since == 0) | anew
    size = np.where(head, np.where(anew, 2.0 ** -7, 2.0 ** 21), np.exp2(5.0 - since))[..., None, None] * np.where(kind == 2, 0.0625, 1.0)
    high = np.sign(h) * (np.abs(h) // 16 * 16)
    upper = np.where(head[..., None, None], h - high, high)
    w = np.argsort(rng.random((N, 8, C)), axis=2)
    g = np.arange(8)[:, None]
    c = S * np.arange(N)[:, None, None] + w % S
    p = np.concatenate([0.0 - digits(C - 1 - c)[..., None, :], 0.0 - digits(C - 1 - i + 0 * c)[..., None, :], upper * size, (h - upper) * size], axis=3)
    q, z = np.zeros(p.shape), np.zeros(p.shape)
    q[w // S, g, c] = p
    z[np.arange(N)[:, None, None], g, np.argsort(rng.random((N, 8, C)), axis=2)] = q
    x = d["x"].astype(np.float32).reshape(N, 8, 16, C, 4)
    x[:, :, np.r_[0:2, 8:16]] = z.transpose(0, 1, 3, 2, 4)
    u, v = d["u"].reshape(N, 128, 128, 4), d["v"].reshape(N, 128, 128, 4)
    u[:, :, ::16] = 0
    v[:, :, ::16] = 0
    for b in range(0, 128, 16):
        u[:, b, b, :3] = -1
        v[:, b + 1, b, :3] = -1
    return {"x": x.reshape(N, 128, 4 * C).astype(BF), "u": u.reshape(N, 128, 512), "v": v.reshape(N, 128, 512), "m": d["m"], **unit(rng, 256, 256, True)}
def setup_inputs_spread(rng):
    d = setup_inputs(rng)
    x = wide(rng, N, 128, 4 * C).astype(np.float32).reshape(N, 128, C, 4)
    x = x * np.exp2(rng.integers(-6, 7, (N, 1, C, 1))).astype(np.float32)
    for r in range(N): x[r][:, rng.permutation(C)[:24 // N]] = 0
    d["x"] = mx_ref.flush(x.reshape(N, 128, 4 * C).astype(BF))
    return d
def scanned(x, u, v, wc, ws):
    first, second, out, value = [], [], [], []
    run = np.arange(S)
    for r in range(N):
        o = order(mx_ref.matmul(mx_ref.quantize(u[r]), mx_ref.quantize(x[r])))
        first.append(o)
        out.append(mx_ref.quantize(gcols(x[r], o)))
    for d in range(N):
        w = pk(wc[d], ws[d])
        a = join(*[pick(out[r], S * d + run) for r in range(N)])
        h = tile([mx_ref.matmul(pick(w, np.arange(128 * b, 128 * b + 128)), a) * np.float32(0.00390625) for b in range(4)])
        o = order(mx_ref.matmul(mx_ref.quantize(v[d]), mx_ref.quantize(h)))
        second.append(o)
        s = gcols(h, o).astype(np.float32).reshape(128, C, 4)
        s[:, 0] = np.maximum(s[:, 0], np.float32(0.0))
        for i in range(1, C): s[:, i] = np.maximum(s[:, i - 1] * np.float32(0.5), s[:, i])
        value.append(s + np.float32(0.0))
    return first, second, value
def check_inputs(d):
    b = []
    for k in ("x", "u", "v", "m"):
        a = np.abs(d[k].astype(np.float32))
        if not (np.isfinite(a).all() and ((a == 0) | (a >= 2.0 ** -30) & (a <= 2.0 ** 30)).all()): b.append("a value of " + k)
    return b
def reference(x, u, v, m, wc, ws):
    first, second, value = scanned(x, u, v, wc, ws)
    back = [mx_ref.quantize(gcols(value[d].reshape(128, 4 * C).astype(BF), places(second[d]))) for d in range(N)]
    run = np.arange(S)
    y, oa, ob = np.zeros((N, 128, C), np.float32), np.zeros((N, 8, C), np.float32), np.zeros((N, 8, C), np.float32)
    oc, osc = np.zeros((N, 128, 4 * C), np.uint8), np.zeros((N, 16, C), np.uint8)
    for r in range(N):
        b = decode(join(*[pick(back[d], S * r + run) for d in range(N)])).astype(BF)
        z = gcols(b, places(first[r])).astype(np.float32) + x[r].astype(np.float32)
        q = mx_ref.quantize(z.astype(BF))
        y[r] = mx_ref.matmul(mx_ref.quantize(m[r]), q)
        oa[r], ob[r] = first[r], second[r]
        oc[r], osc[r] = emit(q)
    return {"y": y, "oa": oa, "ob": ob, "oc": oc, "osc": osc}

@@ -1,0 +1,492 @@
+from concourse.bass import DstId, RemoteDMATransfer
+from concourse.mybir import dt, AluOpType, ActivationFunctionType
+
+ALU = AluOpType
+ACT = ActivationFunctionType
+N, C, S = 8, 384, 48
+H = C // 2
+KB = C // 16
+KH = KB // 2
+AE, AL = 5, 6
+KA = AE + AL
+KV = KB - KA
+TW = 2 * H + 32
+AHEAD = 3
+SGW = C + 8
+
+CODE, PLANE, BF, F32, U16, I32 = "float8_e4m3fn_x4", "uint8", "bfloat16", "float32", "uint16", "int32"
+SCRATCH = {}
+
+
+def _sb(name, cols, dtype):
+    SCRATCH[name] = ("sbuf", [128, cols], dtype)
+
+
+for _n, _c in (("xs", 4 * C), ("us", 512), ("vs", 512), ("ms", 512), ("ft", 4 * C), ("ht", 4 * C), ("hs", 4 * C), ("ss", 4 * C),
+               ("tt", 4 * C), ("zs", 4 * C), ("zt", 4 * C), ("et", 2048), ("mi", C), ("mask", C), ("num", C), ("half", C)):
+    _sb(_n, _c, BF)
+for _n, _c in (("xq", C), ("uq", 128), ("up", 128), ("vq", 128), ("vp", 128), ("mq", 128), ("wq", 512), ("eq4", 512), ("fq", C),
+               ("aq", C), ("hq", C), ("tq", C), ("bq", C), ("zq", C), ("r1", 2 * S), ("r2", 2 * S)):
+    _sb(_n + "c", _c, CODE)
+    _sb(_n + "s", _c, PLANE)
+for _t in "12":
+    _sb("row" + _t, C + 32, F32)
+    _sb("trf" + _t, 2 * TW, F32)
+    _sb("thr" + _t, 32, F32)
+    _sb("same" + _t, C, BF)
+    _sb("later" + _t, C, BF)
+    _sb("init" + _t, 16, BF)
+    _sb("cmp" + _t, KV * C, BF)
+    _sb("sum" + _t, KV * H, BF)
+    _sb("sg" + _t, KA * SGW, F32)
+    _sb("acc" + _t, 2 * KA, F32)
+    _sb("plf" + _t, 16, F32)
+    _sb("pl" + _t, KB, U16)
+    _sb("ord" + _t, C + 32, BF)
+    _sb("trb" + _t, 2 * C + 32, BF)
+    _sb("l4" + _t, 128, U16)
+    _sb("of" + _t, C, F32)
+for _n, _c, _d in (("i8", 8, I32), ("pick", 8, U16), ("i24", KB, I32), ("kl", KB, U16), ("pi", 1, I32), ("b0", 1, I32), ("b1", 1, I32),
+                   ("b2", 1, I32), ("sf", 1, F32), ("e1", 1, F32), ("e2", 1, F32), ("c2", 2, F32), ("k2", 2, F32), ("tl", 2, U16),
+                   ("k15", KB, F32), ("e3", 1, F32), ("k3", 2, F32), ("tl2", 2, U16), ("idn", 128, F32), ("y0", H, F32), ("y1", H, F32)):
+    _sb(_n, _c, _d)
+for _b in range(8):
+    SCRATCH["ps%d" % _b] = ("psum", [128, 512], F32)
+
+SEMAPHORES = ["cv", "ca", "ct", "cp", "lu", "lxa", "lxb", "lv", "lm", "lw", "own1", "own2", "far1", "far2", "near1", "near2",
+              "hc1", "hs1", "hc2", "hs2", "sent", "st", "sta"]
+STAGES = (("fq", "r1", "aq", "1"), ("tq", "r2", "bq", "2"))
+
+
+def bits(engines):
+    m = 0
+    for e in engines:
+        m |= 1 << e
+    return m
+
+
+def words(view):
+    return view.bitcast(dt.uint8)
+
+
+def plan_of(r, T, topo):
+    me = T.cores[r]
+    free = [c for c in topo.cores_of(me) if T.rank_of(c) is None and topo.die(c) != topo.die(me)]
+    hf = r // (N // 2)
+    pairs = []
+    for i in range(2):
+        m = 2 * (1 - hf) + (r // 2 + i) % 2
+        ds = [2 * m, 2 * m + 1]
+        c = [c for c in free if all(topo.may_write(c, T.cores[d]) for d in ds)][0]
+        free.remove(c)
+        pairs.append((c, ds))
+    mine = [d for d in range(hf * N // 2, (hf + 1) * N // 2) if d != r]
+    mine.sort(key=lambda d: (not topo.mates(me, T.cores[d]), topo.same_plane(me, T.cores[d])))
+    return mine, pairs
+
+
+def transfer(topo, src_core, dst_core, engines, sem, src, dst):
+    rid, pid = topo.addr(dst_core, src_core)
+    return RemoteDMATransfer(dst_ids=[DstId(rid=rid, pnc=pid)], dma_engine_mask=bits(engines), remote_sem=sem, src=src, dst=dst)
+
+
+def cols(T, name, kind, a, b):
+    v = T[name + kind][:, a:b]
+    return words(v) if kind == "c" else v
+
+
+def helper_program(g, core, T, topo):
+    for r in range(N):
+        for c, ds in plan_of(r, T, topo)[1]:
+            if c != core:
+                continue
+            sent = 0
+            for src, rel, dst, t in STAGES:
+                for kind in "cs":
+                    g.wait_ge(T.sem["h" + kind + t], 8 if kind == "c" else 4)
+                    ts = []
+                    for i, d in enumerate(ds):
+                        ts.append(transfer(topo, core, T.cores[d], topo.engines(core, T.cores[d])[4 * i:4 * i + 4], T.sem["far" + t],
+                                           cols(T, rel, kind, S * i, S * i + S), cols(T, dst, kind, S * r, S * r + S)))
+                        sent += 4
+                    g.remote_dma_fused(ts, local_sem=T.sem.sent)
+            g.wait_ge(T.sem.sent, sent)
+
+
+def rank_program(g, core, T, topo):
+    rank = T.rank_of(core)
+    if rank is None:
+        helper_program(g, core, T, topo)
+        return
+    Q = {"v": g.vector, "a": g.scalar, "t": g.tensor, "p": g, "s": g.sync}
+    V, A, PE = g.vector, g.scalar, g.tensor
+    cnt = {}
+    seen = {q: {} for q in Q}
+
+    def wait(q, toks):
+        need = {}
+        for s, n in toks:
+            need[s] = max(need.get(s, 0), n)
+        for s in need:
+            if seen[q].get(s, 0) < need[s]:
+                Q[q].wait_ge(T.sem[s], need[s])
+                seen[q][s] = need[s]
+
+    def op(q, call, *after):
+        wait(q, after)
+        s = "c" + q
+        cnt[s] = cnt.get(s, 0) + 1
+        call().then_inc(T.sem[s], 1)
+        return (s, cnt[s])
+
+    def dma(q, s, out, in_, *after):
+        wait(q, after)
+        cnt[s] = cnt.get(s, 0) + 16
+        Q[q].dma_start(out, in_).then_inc(T.sem[s], 16)
+        return (s, cnt[s])
+
+    def quant(name, tile, a, b, *after):
+        return op("v", lambda: V.quantize_mx(T[name + "c"][:, a:b], T[name + "s"][:, a:b], tile[:, 4 * a:4 * b]), *after)
+
+    def mm(bank, w, a, x, c, d, *after):
+        return op("t", lambda: PE.matmul_mx(T["ps%d" % bank][:, 0:d - c], T[w + "c"][:, a:a + 128], T[w + "s"][:, a:a + 128],
+                                            T[x + "c"][:, c:d], T[x + "s"][:, c:d], True, True), *after)
+
+    def ts(out, in0, s1, s2, o0, o1, *after):
+        if o1 is None:
+            return op("v", lambda: V.tensor_scalar(out, in0, s1, None, o0), *after)
+        return op("v", lambda: V.tensor_scalar(out, in0, s1, s2, o0, o1), *after)
+
+    def take(q, out, win, off, *after):
+        if q == "v":
+            return op("v", lambda: V.tensor_copy(out, win.indirect(off)), *after)
+        return op("a", lambda: A.activation(out, win.indirect(off), ACT.Copy), *after)
+
+    def iota(out, pattern, base, cm, whole):
+        if whole:
+            return op("p", lambda: g.iota(out, pattern, base, cm))
+        return op("p", lambda: g.iota(out, pattern, base, cm, allow_small_or_imprecise_dtypes=True))
+
+    hl = rank // (N // 2)
+    he = 1 - hl
+
+    lu = dma("a", "lu", T.us[:], T.u[:])
+    lxa = dma("s", "lxa", T.xs[:, 0:4 * H], T.x[:, 0:4 * H])
+    lxb = dma("s", "lxb", T.xs[:, 4 * H:4 * C], T.x[:, 4 * H:4 * C])
+    dma("s", "lw", words(T.wqc[:]), T.wc[:], lu, lxa, lxb)
+    lw = dma("s", "lw", T.wqs[:], T.ws[:])
+    lv = dma("s", "lv", T.vs[:], T.v[:])
+    lm = dma("s", "lm", T.ms[:], T.m[:])
+
+    i8 = iota(T.i8[:], [[16, 8]], 0, 0, True)
+    pi = iota(T.pi[:], [[1, 1]], 0, 1, True)
+    c2 = iota(T.c2[:], [[16, 2]], 0, 0, False)
+    i24 = iota(T.i24[:], [[1, KB]], 0, 0, True)
+    k15 = iota(T.k15[:], [[16, KB]], 15, 0, False)
+    mi = iota(T.mi[:], [[0, KB], [1, 16]], 0, 0, False)
+    num = iota(T.num[:], [[1, C]], -H, 0, False)
+    idn = iota(T.idn[:], [[1, 128]], 0, -1, False)
+
+    def margins(t):
+        return [op("v", lambda: V.memset(T["row" + t][:, 0:16], 0.0)), op("v", lambda: V.memset(T["row" + t][:, C + 16:C + 32], 0.0)),
+                op("v", lambda: V.memset(T["row" + t][:, H:H + 32], 0.0)), op("v", lambda: V.memset(T["ord" + t][:], 0.0))]
+
+    pads = {"1": margins("1")}
+    pick = op("v", lambda: V.tensor_copy(T.pick[:], T.i8[:]), i8)
+    b0 = ts(T.b0[:], T.pi[:], 15, None, ALU.bitwise_and, None, pi)
+    b1 = ts(T.b1[:], T.pi[:], 1, None, ALU.bitwise_and, None)
+    b2 = ts(T.b2[:], T.pi[:], 4, 1, ALU.logical_shift_right, ALU.bitwise_and)
+    sf = op("v", lambda: V.tensor_copy(T.sf[:], T.b0[:]), b0)
+    e1 = op("v", lambda: V.tensor_tensor(T.e1[:], T.b1[:], T.b2[:], ALU.is_equal), b1, b2)
+    k2 = ts(T.k2[:], T.c2[:], T.sf[:], float(KB - 1), ALU.add, ALU.min, sf, c2)
+    k3 = ts(T.k3[:], T.c2[:], T.sf[:], float(KH - 1), ALU.add, ALU.min)
+    e2 = ts(T.e2[:], T.e1[:], float(C + 16), 16.0, ALU.mult, ALU.add, e1)
+    e3 = ts(T.e3[:], T.e1[:], float(H + 16), 16.0, ALU.mult, ALU.add)
+    kl = op("v", lambda: V.tensor_copy(T.kl[:], T.i24[:]), i24)
+    tl = ts(T.tl[:], T.k2[:], 16.0, T.e2[:], ALU.mult, ALU.add, k2, e2)
+    tl2 = ts(T.tl2[:], T.k3[:], 16.0, T.e3[:], ALU.mult, ALU.add, k3, e3)
+
+    def sixteen(q, p, tok):
+        a = op("v", lambda: V.tensor_copy(T[p + "c"][:].bitcast(dt.uint32), T[q + "c"][:].bitcast(dt.uint32).indirect(T.pick[:])), tok, pick)
+        b = take("a", T[p + "s"][:], T[q + "s"][:], T.pick[:], tok, pick)
+        return a, b
+
+    def sorter(t, hf, mask):
+        row, trf, thr, sg, acc, pl = T["row" + t], T["trf" + t], T["thr" + t], T["sg" + t], T["acc" + t], T["pl" + t]
+        cmp_, sm, od, trb, later, init = T["cmp" + t], T["sum" + t], T["ord" + t], T["trb" + t], T["later" + t], T["init" + t]
+        lo = KH - (AL if hf else AE)
+        st = {}
+
+        def of_half(h, scalar):
+            return [k for k in range(KH * h, KH * h + KH) if (lo <= k < lo + KA) == scalar]
+
+        def slot(k):
+            return k if k < lo else k - KA
+
+        def own(k):
+            c = 16 * (k // KH) + k % KH
+            return thr[:, c:c + 1]
+
+        def scores(w, x, h, banks, *after):
+            pa = mm(banks[0], w, 0, x, H * h, H * h + H, *after)
+            pv = mm(banks[1], w, 0, x, H * h, H * h + H)
+            before = [st["t1"]] if "t1" in st else pads[t]
+            r = op("a", lambda: A.activation(row[:, 16 + H * h:16 + H * h + H], T["ps%d" % banks[0]][:, 0:H], ACT.Copy), pa, *before)
+            st["pv"], st["r", h] = pv, r
+            st["banks"] = banks
+
+        def owns(h):
+            t2 = op("v", lambda: V.transpose(trf[:, TW * h + H + 32:TW * h + TW], T["ps%d" % st["banks"][1]][:, 0:H]), st["pv"])
+            st["t1"] = op("v", lambda: V.transpose(trf[:, TW * h:TW * h + H + 32], row[:, H * h:H * h + H + 32]), st["r", h])
+            st["th", h] = take("v", thr[:, 16 * h:16 * h + 16], trf[:, TW * h:TW * h + TW], T.tl2[:, 0:1], tl2, st["t1"], t2)
+
+        def compare(k, a, b, *after):
+            n, c = 16 * k + 16, C * slot(k)
+            for x, y, how in ((a, min(b, n), ALU.is_ge), (max(a, n), b, ALU.is_gt)):
+                if x < y:
+                    st["cm", k] = ts(cmp_[:, c + x:c + y], row[:, 16 + x:16 + y], own(k), None, how, None, st["th", k // KH], *after)
+
+        def ties(h, fill):
+            a, b = H * h, H * h + H
+            same = op("v", lambda: V.tensor_tensor(T["same" + t][:, a:b], thr[:, 16 * h:16 * h + 16].indirect(T.kl[:, 0:KH]), row[:, 16 + a:16 + b], ALU.is_equal),
+                      st["th", h], kl)
+            fill[0]()
+            lt = op("v", lambda: V.tensor_tensor_scan(later[:, a:b], T["same" + t][:, a:b], T.mask[:, a:b], 0.0, ALU.add, ALU.mult), same, mask)
+            fill[1]()
+            ks = of_half(h, True)
+            st["wa", h] = op("v", lambda: V.tensor_tensor(sg[:, SGW * (ks[0] - lo) + C:SGW * (ks[-1] - lo + 1):SGW], later[:, 16 * ks[0] + 15:16 * ks[-1] + 16:16],
+                                                          T.k15[:, ks[0]:ks[-1] + 1], ALU.subtract), lt, k15)
+            ks = of_half(h, False)
+            st["wd", h] = ts(init[:, slot(ks[0]):slot(ks[-1]) + 1], later[:, 16 * ks[0] + 15:16 * ks[-1] + 16:16], -1.0, -1.0 - H, ALU.mult, ALU.add)
+
+        def total(k):
+            c = slot(k)
+            st["sum", k] = op("v", lambda: V.tensor_tensor_scan(sm[:, H * c:H * c + H], cmp_[:, C * c:C * c + H], cmp_[:, C * c + H:C * c + C],
+                                                                init[:, c:c + 1], ALU.add, ALU.add), st["cm", k], st["wd", k // KH])
+
+        def sign(k, a, b, *after):
+            c = SGW * (k - lo)
+            st["sn", k] = op("a", lambda: A.activation(sg[:, c + a:c + b], row[:, 16 + a:16 + b], ACT.Sign, bias=own(k), scale=-1.0), st["th", k // KH], *after)
+
+        def smaller(k):
+            i, n = k - lo, 16 * k + 16
+            v = sg[:, SGW * i:SGW * i + n]
+            st["done", k] = op("a", lambda: A.activation(v, v, ACT.Relu, accum_out=acc[:, i:i + 1]), st["sn", k])
+
+        def larger(k):
+            i, n = k - lo, 16 * k + 16
+            v = sg[:, SGW * i + n:SGW * i + C + 1]
+            st["done", k] = op("a", lambda: A.activation(v, v, ACT.Relu, scale=-1.0, accum_out=acc[:, KA + i:KA + i + 1]), st["sn", k], st["wa", k // KH])
+
+        a1, z1, a2, z2 = H * hf, H * hf + H, H * (1 - hf), H * (1 - hf) + H
+
+        def first_vector(ks):
+            for k in ks:
+                compare(k, a1, z1)
+
+        def first():
+            owns(hf)
+            ks = of_half(hf, False)
+            ties(hf, [lambda: compare(ks[0], a1, z1), lambda: compare(ks[1], a1, z1)])
+            ka = of_half(hf, True)
+            for k in ka:
+                sign(k, a1, z1)
+            for k in ka:
+                (larger if hf else smaller)(k)
+            return ks[2:]
+
+        def places(h):
+            ka, kv = of_half(h, True), of_half(h, False)
+            a, b = ka[0] - lo, ka[-1] - lo + 1
+            d = op("v", lambda: V.tensor_tensor(T["plf" + t][:, a:b], acc[:, KA + a:KA + b], acc[:, a:b], ALU.subtract), st["done", ka[0]], st["done", ka[-1]])
+            p0 = ts(pl[:, kv[0]:kv[-1] + 1], sm[:, H * slot(kv[0]) + H - 1:H * slot(kv[-1]) + H:H], float(H), None, ALU.add, None, st["sum", kv[-1]])
+            p1 = op("v", lambda: V.tensor_copy(pl[:, ka[0]:ka[-1] + 1], T["plf" + t][:, a:b]), d)
+            before = [st["sc"]] if "sc" in st else pads[t]
+            st["sc"] = op("v", lambda: V.tensor_copy(od[:, 16:C + 16].indirect(pl[:, KH * h:KH * h + KH]), T.num[:, H * h:H * h + H]), p0, p1, num, *before)
+            return p1
+
+        def second():
+            h = 1 - hf
+            r = st["r", h]
+            ke, kv = of_half(hf, False), of_half(h, False)
+            for k in of_half(hf, True):
+                sign(k, a2, z2, r)
+            owns(h)
+            ties(h, [lambda: compare(ke[0], a2, z2, r), lambda: compare(ke[1], a2, z2, r)])
+            for k in of_half(hf, True):
+                (smaller if hf else larger)(k)
+            ka = of_half(h, True)
+            for k in ka[:AHEAD]:
+                sign(k, 0, C)
+            for i, k in enumerate(ka):
+                if i + AHEAD < len(ka):
+                    sign(ka[i + AHEAD], 0, C)
+                smaller(k)
+                larger(k)
+            todo = ke[:2]
+            for k in ke[2:] + kv:
+                if k in ke:
+                    compare(k, a2, z2)
+                else:
+                    compare(k, 0, C)
+                total(todo.pop(0))
+                todo.append(k)
+            for k in todo:
+                total(k)
+            places(hf)
+            p = places(h)
+            u1 = op("v", lambda: V.transpose(trb[:, 0:C + 32], od[:]), st["sc"])
+            u2 = op("v", lambda: V.transpose(trb[:, C + 32:2 * C + 32], od[:, 16:C + 16]))
+            lists = {}
+            for b in (1, 3, 0, 2):
+                lists[b] = ts(T["l4" + t][:, 32 * b:32 * b + 32], trb[:].indirect(T.tl[:]), 4.0, 4.0 * H + b, ALU.mult, ALU.add, u1, u2, tl)
+            return lists, p, st["sc"]
+
+        return scores, first, first_vector, second
+
+    def write_order(t, out, tok):
+        f = op("a", lambda: A.activation(T["of" + t][:], T["ord" + t][:, 16:C + 16], ACT.Identity, bias=float(H)), tok)
+        for k in range(8):
+            dma("s", "st", out[k:k + 1, :], T["of" + t][16 * k:16 * k + 1, :], f)
+
+    mine, pairs = plan_of(rank, T, topo)
+    off = topo.engines(core, T.cores[mine[0]])
+    cnt["sent"] = 0
+
+    def leave_early(stage, tok):
+        src, rel, dst, t = STAGES[stage]
+        wait("p", [tok])
+        for kind in "cs":
+            tr = []
+            for i, (c, ds) in enumerate(pairs):
+                eng = topo.engines(core, c)
+                eng = eng[8 * i:8 * i + 8] if kind == "c" else [e for e in eng if e not in off][4 * i:4 * i + 4]
+                tr.append(transfer(topo, core, c, eng, T.sem["h" + kind + t],
+                                   cols(T, src, kind, S * ds[0], S * ds[0] + 2 * S), cols(T, rel, kind, 0, 2 * S)))
+                cnt["sent"] += len(eng)
+            g.remote_dma_fused(tr, local_sem=T.sem.sent)
+        cnt["far" + t] = 2 * 4 * 4
+        return ("far" + t, cnt["far" + t])
+
+    def leave_late(stage, tok):
+        src, rel, dst, t = STAGES[stage]
+        wait("p", [tok])
+        deal = {"c": (off[0:4], off[4:6], off[6:8]), "s": (off[0:2], off[2:4], off[4:8])}
+        for kind in "cs":
+            tr = []
+            for d, eng in zip(mine, deal[kind]):
+                tr.append(transfer(topo, core, T.cores[d], eng, T.sem["near" + t],
+                                   cols(T, src, kind, S * d, S * d + S), cols(T, dst, kind, S * rank, S * rank + S)))
+            g.remote_dma_fused(tr, local_sem=T.sem.sent)
+            cnt["sent"] += 8
+        for kind in "cs":
+            own = dma("s", "own" + t, cols(T, dst, kind, S * rank, S * rank + S), cols(T, src, kind, S * rank, S * rank + S), tok)
+        cnt["near" + t] = 16
+        return own, ("near" + t, 16)
+
+    qu = quant("uq", T.us, 0, 128, lu)
+    up = sixteen("uq", "up", qu)
+    mask = ts(T.mask[:], T.mi[:], T.sf[:], None, ALU.is_gt, None, mi, sf)
+    scores, first, first_vector, second = sorter("1", 0, mask)
+    scores("up", "xq", 0, (0, 1), quant("xq", T.xs, 0, H, lxa), *up)
+    left = first()
+    scores("up", "xq", 1, (2, 3), quant("xq", T.xs, H, C, lxb))
+    first_vector(left)
+    lists, pl1, ord1 = second()
+
+    def part(q, b, h):
+        a = 32 * b + KH * h
+        return take(q, T.ft[:, 4 * H * h + b:4 * H * (h + 1):4], T.xs[:], T.l41[:, a:a + KH], lists[b], lxa, lxb)
+
+    got = [part("a", 1, he), part("a", 3, he), part("v", 0, he), part("v", 2, he)]
+    early = leave_early(0, quant("fq", T.ft, H * he, H * he + H, *got))
+    got = [part("a", 1, hl), part("a", 3, hl), part("v", 0, hl), part("a", 2, hl)]
+    qf = quant("fq", T.ft, H * hl, H * hl + H, *got)
+    late = leave_late(0, qf)
+
+    qv = quant("vq", T.vs, 0, 128, lv)
+    pads["2"] = margins("2")
+    half = op("v", lambda: V.memset(T.half[:], 0.5))
+    vp = sixteen("vq", "vp", qv)
+    write_order("1", T.oa, ord1)
+    ze = op("v", lambda: V.memset(T.et[:], 0.0))
+
+    def layer(h, banks, *after):
+        rs = [mm(banks[b], "wq", 128 * b, "aq", H * h, H * h + H, lw, qf, *after) for b in (1, 0, 3, 2)]
+        got = []
+        for b, tok in zip((1, 0, 3, 2), rs):
+            out, ps = T.ht[:, 4 * H * h + b:4 * H * (h + 1):4], T["ps%d" % banks[b]][:, 0:H]
+            if b % 2:
+                got.append(op("a", lambda: A.activation(out, ps, ACT.Copy, scale=0.00390625), tok))
+            else:
+                got.append(ts(out, ps, 0.00390625, None, ALU.mult, None, tok))
+        return quant("hq", T.ht, H * h, H * h + H, *got)
+
+    scores, first, first_vector, second = sorter("2", hl, mask)
+    qe = layer(hl, (0, 1, 2, 3), *late)
+    scores("vp", "hq", hl, (4, 5), qe, *vp)
+    left = first()
+    first_vector(left[:-2])
+    qh = layer(he, (6, 7, 0, 1), qe, early)
+    scores("vp", "hq", he, (2, 3), qh)
+    first_vector(left[-2:])
+    lists, pl2, ord2 = second()
+
+    def fwd(q, b):
+        return take(q, T.hs[:, C * b:C * b + C], T.ht[:], T.l42[:, 32 * b:32 * b + KB], lists[b], qh)
+
+    def scan(b, tok):
+        return op("v", lambda: V.tensor_tensor_scan(T.ss[:, C * b:C * b + C], T.half[:], T.hs[:, C * b:C * b + C], 0.0, ALU.mult, ALU.max), tok, half)
+
+    def back(q, out, src, pl, b, h, *after):
+        return take(q, out[:, 4 * H * h + b:4 * H * (h + 1):4], src[:, C * b:C * b + C], pl[:, KH * h:KH * h + KH], *after)
+
+    f1 = fwd("a", 1)
+    f3 = fwd("a", 3)
+    f0 = fwd("v", 0)
+    s1 = scan(1, f1)
+    s0 = scan(0, f0)
+    s3 = scan(3, f3)
+    f2 = fwd("v", 2)
+    s2 = scan(2, f2)
+    sc = (s0, s1, s2, s3)
+    got = [back(q, T.tt, T.ss, T.pl2, b, he, sc[b], pl2) for q, b in (("a", 1), ("a", 0), ("a", 3), ("v", 2))]
+    early = leave_early(1, quant("tq", T.tt, H * he, H * he + H, *got))
+    got = [back(q, T.tt, T.ss, T.pl2, b, hl, sc[b]) for q, b in (("a", 1), ("a", 0), ("a", 3), ("v", 2))]
+    qt = quant("tq", T.tt, H * hl, H * hl + H, *got)
+    late = leave_late(1, qt)
+
+    ones = [ts(T.et[:, 512 * b + b:512 * b + 512:4], T.idn[:], 0.0, None, ALU.is_equal, None, ze, idn) for b in range(4)]
+    qe = quant("eq4", T.et, 0, 512, *ones)
+    qm = quant("mq", T.ms, 0, 128, lm)
+    write_order("2", T.ob, ord2)
+
+    def add(h, bank, *after):
+        ds = [mm(bank + b, "eq4", 128 * b, "bq", H * h, H * h + H, qe, qt, *after) for b in range(4)]
+        return [op("v", lambda: V.tensor_tensor(T.zs[:, C * b + H * h:C * b + H * h + H], T["ps%d" % (bank + b)][:, 0:H],
+                                                T.ft[:, 4 * H * h + b:4 * H * (h + 1):4], ALU.add), ds[b]) for b in range(4)]
+
+    add(hl, 4, *late)
+    sums = add(he, 0, early)
+
+    def home(q, b, h):
+        return back(q, T.zt, T.zs, T.pl1, b, h, sums[b], pl1)
+
+    one = [home("a", 0, 0), home("a", 1, 0), home("a", 2, 0), home("v", 3, 0)]
+    two = [home("a", 0, 1), home("a", 1, 1), home("v", 3, 1)]
+    qz = quant("zq", T.zt, 0, H, *one)
+    y0 = mm(4, "mq", 0, "zq", 0, H, qz, qm)
+    dma("s", "st", T.oc[:, 0:4 * H], words(T.zqc[:, 0:H]), qz)
+    two.append(home("v", 2, 1))
+    c0 = op("a", lambda: A.activation(T.y0[:], T.ps4[:, 0:H], ACT.Copy), y0)
+    dma("s", "st", T.y[:, 0:H], T.y0[:], c0)
+    qz = quant("zq", T.zt, H, C, *two)
+    y1 = mm(5, "mq", 0, "zq", H, C, qz)
+    dma("s", "st", T.oc[:, 4 * H:4 * C], words(T.zqc[:, H:C]), qz)
+    c1 = op("v", lambda: V.tensor_copy(T.y1[:], T.ps5[:, 0:H]), y1)
+    for k in range(4):
+        q = "sa"[k // 2]
+        dma(q, "st" if q == "s" else "sta", T.osc[4 * k:4 * k + 4, :], T.zqs[32 * k:32 * k + 4, :], qz)
+    dma("a", "sta", T.y[:, H:C], T.y1[:], c1)
+
+    wait("p", [(s, cnt[s]) for s in cnt])

@@ -1,18 +1,18 @@
 from concourse.bass import DstId, RemoteDMATransfer
-from concourse.mybir import dt, AluOpType, ActivationFunctionType
+from concourse.mybir import dt, AluOpType as ALU, ActivationFunctionType as ACT
 
-ALU = AluOpType
-ACT = ActivationFunctionType
 N, C, S = 8, 384, 48
 H = C // 2
 KB = C // 16
 KH = KB // 2
-AE, AL = 5, 6
-KA = AE + AL
-KV = KB - KA
 TW = 2 * H + 32
-AHEAD = 3
 SGW = C + 8
+PAR = {"ae1": 5, "al1": 6, "ae2": 5, "al2": 6, "e01": 2, "e02": 5, "ea": 3, "v01": 3, "v02": 7, "pos1": -1, "pos2": 3, "la2": 2,
+       "sa1": 2, "sa2": 2, "nl1": 2, "nl2": 2,
+       "fa": "x1w x3w y1w y3w y2a o", "fv": "u l U m x0w L x2w M q0 y0w y2b q1",
+       "sa": "f1w f3w x1w x0w x3w y1w y0w y3a", "sv": "f0w s1 s0 f2w s3 s2 x2w q0 y2w y3b q1",
+       "adds": "l0 l1 e0 e1 l2 e2 l3 e3", "ha": "00 10 20 01 11 y0 S2 S3 Y1", "hv": "30 q0 31 21 q1 y1", "hs": "C0 Y0 C1 S0 S1"}
+SPAN = {"w": (0, H), "a": (0, H // 2), "b": (H // 2, H)}
 
 CODE, PLANE, BF, F32, U16, I32 = "float8_e4m3fn_x4", "uint8", "bfloat16", "float32", "uint16", "int32"
 SCRATCH = {}
@@ -23,37 +23,26 @@ def _sb(name, cols, dtype):
 
 
 for _n, _c in (("xs", 4 * C), ("us", 512), ("vs", 512), ("ms", 512), ("ft", 4 * C), ("ht", 4 * C), ("hs", 4 * C), ("ss", 4 * C),
-               ("tt", 4 * C), ("zs", 4 * C), ("zt", 4 * C), ("et", 2048), ("mi", C), ("mask", C), ("num", C), ("half", C)):
+               ("tt", 4 * C), ("zs", 4 * C), ("zt", 4 * C), ("et", 2048), ("eo", 2048), ("mi", H), ("mask", H), ("num", C), ("half", C),
+               ("xs1", 4 * C + 16), ("ht1", 4 * C + 16)):
     _sb(_n, _c, BF)
 for _n, _c in (("xq", C), ("uq", 128), ("up", 128), ("vq", 128), ("vp", 128), ("mq", 128), ("wq", 512), ("eq4", 512), ("fq", C),
                ("aq", C), ("hq", C), ("tq", C), ("bq", C), ("zq", C), ("r1", 2 * S), ("r2", 2 * S)):
     _sb(_n + "c", _c, CODE)
     _sb(_n + "s", _c, PLANE)
 for _t in "12":
-    _sb("row" + _t, C + 32, F32)
-    _sb("trf" + _t, 2 * TW, F32)
-    _sb("thr" + _t, 32, F32)
-    _sb("same" + _t, C, BF)
-    _sb("later" + _t, C, BF)
-    _sb("init" + _t, 16, BF)
-    _sb("cmp" + _t, KV * C, BF)
-    _sb("sum" + _t, KV * H, BF)
-    _sb("sg" + _t, KA * SGW, F32)
-    _sb("acc" + _t, 2 * KA, F32)
-    _sb("plf" + _t, 16, F32)
-    _sb("pl" + _t, KB, U16)
-    _sb("ord" + _t, C + 32, BF)
-    _sb("trb" + _t, 2 * C + 32, BF)
-    _sb("l4" + _t, 128, U16)
-    _sb("of" + _t, C, F32)
+    for _n, _c, _d in (("row", C + 32, F32), ("trf", 2 * TW, F32), ("thr", 32, F32), ("same", C, BF), ("later", C, BF),
+                       ("cmp", KB * C, BF), ("sum", KB * H, BF), ("sg", KB * SGW, F32), ("acc", 2 * KB, F32), ("plf", KB, F32), ("pl", KB, U16),
+                       ("ord", C + 32, BF), ("trb", 2 * TW, BF), ("l4", 64, U16), ("of", C, F32)):
+        _sb(_n + _t, _c, _d)
 for _n, _c, _d in (("i8", 8, I32), ("pick", 8, U16), ("i24", KB, I32), ("kl", KB, U16), ("pi", 1, I32), ("b0", 1, I32), ("b1", 1, I32),
-                   ("b2", 1, I32), ("sf", 1, F32), ("e1", 1, F32), ("e2", 1, F32), ("c2", 2, F32), ("k2", 2, F32), ("tl", 2, U16),
-                   ("k15", KB, F32), ("e3", 1, F32), ("k3", 2, F32), ("tl2", 2, U16), ("idn", 128, F32), ("y0", H, F32), ("y1", H, F32)):
+                   ("b2", 1, I32), ("sf", 1, F32), ("e1", 1, F32), ("e2", 1, F32), ("c2", 4, F32), ("k2", 2, F32), ("tl", 2, U16),
+                   ("k15", KB, F32), ("e3", 1, F32), ("k3", 2, F32), ("tl2", 2, U16), ("mine", 4, U16), ("y0", H, F32), ("y1", H, F32)):
     _sb(_n, _c, _d)
 for _b in range(8):
     SCRATCH["ps%d" % _b] = ("psum", [128, 512], F32)
 
-SEMAPHORES = ["cv", "ca", "ct", "cp", "lu", "lxa", "lxb", "lv", "lm", "lw", "own1", "own2", "far1", "far2", "near1", "near2",
+SEMAPHORES = ["cv", "ca", "ct", "cp", "lu", "lxa", "lxb", "lv", "lm", "lw", "lx", "lh", "far1", "far2", "near1", "near2",
               "hc1", "hs1", "hc2", "hs2", "sent", "st", "sta"]
 STAGES = (("fq", "r1", "aq", "1"), ("tq", "r2", "bq", "2"))
 
@@ -95,15 +84,23 @@ def cols(T, name, kind, a, b):
     return words(v) if kind == "c" else v
 
 
+def relay_engines(t, kind, i, eng, off):
+    if t == "2" and kind == "c":
+        return eng[8 * i:8 * i + 8]
+    return [e for e in eng if e not in off][4 * i:4 * i + 4]
+
+
 def helper_program(g, core, T, topo):
     for r in range(N):
-        for c, ds in plan_of(r, T, topo)[1]:
+        mine, pairs = plan_of(r, T, topo)
+        for j, (c, ds) in enumerate(pairs):
             if c != core:
                 continue
             sent = 0
+            me = T.cores[r]
             for src, rel, dst, t in STAGES:
                 for kind in "cs":
-                    g.wait_ge(T.sem["h" + kind + t], 8 if kind == "c" else 4)
+                    g.wait_ge(T.sem["h" + kind + t], len(relay_engines(t, kind, j, topo.engines(me, c), topo.engines(me, T.cores[mine[0]]))))
                     ts = []
                     for i, d in enumerate(ds):
                         ts.append(transfer(topo, core, T.cores[d], topo.engines(core, T.cores[d])[4 * i:4 * i + 4], T.sem["far" + t],
@@ -120,8 +117,10 @@ def rank_program(g, core, T, topo):
         return
     Q = {"v": g.vector, "a": g.scalar, "t": g.tensor, "p": g, "s": g.sync}
     V, A, PE = g.vector, g.scalar, g.tensor
-    cnt = {}
+    cnt = {"sent": 0}
     seen = {q: {} for q in Q}
+    todo = {q: [] for q in Q}
+    done = {"near1": ("near1", 16), "near2": ("near2", 16), "far1": ("far1", 32), "far2": ("far2", 32)}
 
     def wait(q, toks):
         need = {}
@@ -132,361 +131,453 @@ def rank_program(g, core, T, topo):
                 Q[q].wait_ge(T.sem[s], need[s])
                 seen[q][s] = need[s]
 
-    def op(q, call, *after):
-        wait(q, after)
-        s = "c" + q
-        cnt[s] = cnt.get(s, 0) + 1
-        call().then_inc(T.sem[s], 1)
-        return (s, cnt[s])
+    def issue():
+        while any(todo.values()):
+            moved = False
+            for q in Q:
+                while todo[q] and all(a in done for a in todo[q][0][4]):
+                    name, s, step, call, after = todo[q].pop(0)
+                    wait(q, [done[a] for a in after])
+                    if s is None:
+                        call()
+                    else:
+                        cnt[s] = cnt.get(s, 0) + step
+                        call().then_inc(T.sem[s], step)
+                        done[name] = (s, cnt[s])
+                    moved = True
+            assert moved
 
-    def dma(q, s, out, in_, *after):
-        wait(q, after)
-        cnt[s] = cnt.get(s, 0) + 16
-        Q[q].dma_start(out, in_).then_inc(T.sem[s], 16)
-        return (s, cnt[s])
+    def op(q, name, call, *after):
+        todo[q].append((name, "c" + q, 1, call, after))
+        return name
 
-    def quant(name, tile, a, b, *after):
-        return op("v", lambda: V.quantize_mx(T[name + "c"][:, a:b], T[name + "s"][:, a:b], tile[:, 4 * a:4 * b]), *after)
+    def dma(q, s, name, out, in_, *after):
+        todo[q].append((name, s, 16, lambda: Q[q].dma_start(out, in_), after))
+        return name
 
-    def mm(bank, w, a, x, c, d, *after):
-        return op("t", lambda: PE.matmul_mx(T["ps%d" % bank][:, 0:d - c], T[w + "c"][:, a:a + 128], T[w + "s"][:, a:a + 128],
-                                            T[x + "c"][:, c:d], T[x + "s"][:, c:d], True, True), *after)
+    def quant(name, q, tile, a, b, *after):
+        return op("v", name, lambda: V.quantize_mx(T[q + "c"][:, a:b], T[q + "s"][:, a:b], tile[:, 4 * a:4 * b]), *after)
 
-    def ts(out, in0, s1, s2, o0, o1, *after):
+    def mm(name, bank, w, a, x, c, d, *after):
+        return op("t", name, lambda: PE.matmul_mx(T["ps%d" % bank][:, 0:d - c], T[w + "c"][:, a:a + 128], T[w + "s"][:, a:a + 128],
+                                                  T[x + "c"][:, c:d], T[x + "s"][:, c:d], True, True), *after)
+
+    def ts(name, out, in0, s1, s2, o0, o1, *after):
         if o1 is None:
-            return op("v", lambda: V.tensor_scalar(out, in0, s1, None, o0), *after)
-        return op("v", lambda: V.tensor_scalar(out, in0, s1, s2, o0, o1), *after)
+            return op("v", name, lambda: V.tensor_scalar(out, in0, s1, None, o0), *after)
+        return op("v", name, lambda: V.tensor_scalar(out, in0, s1, s2, o0, o1), *after)
 
-    def take(q, out, win, off, *after):
+    def tt(name, out, in0, in1, how, *after):
+        return op("v", name, lambda: V.tensor_tensor(out, in0, in1, how), *after)
+
+    def scan(name, out, d0, d1, first, o0, o1, *after):
+        return op("v", name, lambda: V.tensor_tensor_scan(out, d0, d1, first, o0, o1), *after)
+
+    def copy(name, out, in_, *after):
+        return op("v", name, lambda: V.tensor_copy(out, in_), *after)
+
+    def turn(name, out, in_, *after):
+        return op("v", name, lambda: V.transpose(out, in_), *after)
+
+    def fill(name, out, value, *after):
+        return op("v", name, lambda: V.memset(out, value), *after)
+
+    def act(name, out, in_, func, *after, **kw):
+        return op("a", name, lambda: A.activation(out, in_, func, **kw), *after)
+
+    def take(q, name, out, win, off, *after):
         if q == "v":
-            return op("v", lambda: V.tensor_copy(out, win.indirect(off)), *after)
-        return op("a", lambda: A.activation(out, win.indirect(off), ACT.Copy), *after)
+            return copy(name, out, win.indirect(off), *after)
+        return act(name, out, win.indirect(off), ACT.Copy, *after)
 
-    def iota(out, pattern, base, cm, whole):
+    def iota(name, pattern, base, cm, whole):
         if whole:
-            return op("p", lambda: g.iota(out, pattern, base, cm))
-        return op("p", lambda: g.iota(out, pattern, base, cm, allow_small_or_imprecise_dtypes=True))
+            return op("p", name, lambda: g.iota(T[name][:], pattern, base, cm))
+        return op("p", name, lambda: g.iota(T[name][:], pattern, base, cm, allow_small_or_imprecise_dtypes=True))
 
     hl = rank // (N // 2)
     he = 1 - hl
 
-    lu = dma("a", "lu", T.us[:], T.u[:])
-    lxa = dma("s", "lxa", T.xs[:, 0:4 * H], T.x[:, 0:4 * H])
-    lxb = dma("s", "lxb", T.xs[:, 4 * H:4 * C], T.x[:, 4 * H:4 * C])
-    dma("s", "lw", words(T.wqc[:]), T.wc[:], lu, lxa, lxb)
-    lw = dma("s", "lw", T.wqs[:], T.ws[:])
-    lv = dma("s", "lv", T.vs[:], T.v[:])
-    lm = dma("s", "lm", T.ms[:], T.m[:])
+    dma("a", "lu", "lu", T.us[:], T.u[:])
+    dma("s", "lxa", "lxa", T.xs[:, 0:4 * H], T.x[:, 0:4 * H])
+    dma("s", "lxb", "lxb", T.xs[:, 4 * H:4 * C], T.x[:, 4 * H:4 * C])
+    dma("s", "lx", "lx1", T.xs1[:, 15:15 + 4 * C], T.x[:], "lu", "lxa", "lxb")
+    dma("s", "lw", "lw0", words(T.wqc[:]), T.wc[:])
+    dma("s", "lw", "lw", T.wqs[:], T.ws[:])
+    dma("s", "lv", "lv", T.vs[:], T.v[:])
+    dma("s", "lm", "lm", T.ms[:], T.m[:])
 
-    i8 = iota(T.i8[:], [[16, 8]], 0, 0, True)
-    pi = iota(T.pi[:], [[1, 1]], 0, 1, True)
-    c2 = iota(T.c2[:], [[16, 2]], 0, 0, False)
-    i24 = iota(T.i24[:], [[1, KB]], 0, 0, True)
-    k15 = iota(T.k15[:], [[16, KB]], 15, 0, False)
-    mi = iota(T.mi[:], [[0, KB], [1, 16]], 0, 0, False)
-    num = iota(T.num[:], [[1, C]], -H, 0, False)
-    idn = iota(T.idn[:], [[1, 128]], 0, -1, False)
+    iota("i8", [[16, 8]], 0, 0, True)
+    iota("pi", [[1, 1]], 0, 1, True)
+    iota("c2", [[16, 4]], 0, 0, False)
+    iota("i24", [[1, KB]], 0, 0, True)
+    iota("k15", [[16, KB]], 15, 0, False)
+    iota("mi", [[0, KH], [1, 16]], 0, 0, False)
+    iota("num", [[1, C]], -H, 0, False)
+    op("p", "half", lambda: g.affine_select(T.half[:], T.num[:], [[0, C]], ALU.is_gt, 0.5, 0, 0), "num")
+    iota("eo", [[0, 2048]], 1, 0, False)
+    op("p", "et", lambda: g.affine_select(T.et[:], T.eo[:], [[-1, 4], [1, 512]], ALU.is_equal, 0.0, 0, -4), "eo")
 
     def margins(t):
-        return [op("v", lambda: V.memset(T["row" + t][:, 0:16], 0.0)), op("v", lambda: V.memset(T["row" + t][:, C + 16:C + 32], 0.0)),
-                op("v", lambda: V.memset(T["row" + t][:, H:H + 32], 0.0)), op("v", lambda: V.memset(T["ord" + t][:], 0.0))]
+        fill("padA" + t, T["row" + t][:, 0:16], 0.0)
+        fill("padB" + t, T["row" + t][:, C + 16:C + 32], 0.0)
+        fill("padC" + t, T["row" + t][:, H:H + 32], 0.0)
+        fill("padD" + t, T["ord" + t][:, 0:16], 0.0)
+        fill("padE" + t, T["ord" + t][:, C + 16:C + 32], 0.0)
 
-    pads = {"1": margins("1")}
-    pick = op("v", lambda: V.tensor_copy(T.pick[:], T.i8[:]), i8)
-    b0 = ts(T.b0[:], T.pi[:], 15, None, ALU.bitwise_and, None, pi)
-    b1 = ts(T.b1[:], T.pi[:], 1, None, ALU.bitwise_and, None)
-    b2 = ts(T.b2[:], T.pi[:], 4, 1, ALU.logical_shift_right, ALU.bitwise_and)
-    sf = op("v", lambda: V.tensor_copy(T.sf[:], T.b0[:]), b0)
-    e1 = op("v", lambda: V.tensor_tensor(T.e1[:], T.b1[:], T.b2[:], ALU.is_equal), b1, b2)
-    k2 = ts(T.k2[:], T.c2[:], T.sf[:], float(KB - 1), ALU.add, ALU.min, sf, c2)
-    k3 = ts(T.k3[:], T.c2[:], T.sf[:], float(KH - 1), ALU.add, ALU.min)
-    e2 = ts(T.e2[:], T.e1[:], float(C + 16), 16.0, ALU.mult, ALU.add, e1)
-    e3 = ts(T.e3[:], T.e1[:], float(H + 16), 16.0, ALU.mult, ALU.add)
-    kl = op("v", lambda: V.tensor_copy(T.kl[:], T.i24[:]), i24)
-    tl = ts(T.tl[:], T.k2[:], 16.0, T.e2[:], ALU.mult, ALU.add, k2, e2)
-    tl2 = ts(T.tl2[:], T.k3[:], 16.0, T.e3[:], ALU.mult, ALU.add, k3, e3)
+    margins("1")
+    copy("pick", T.pick[:], T.i8[:], "i8")
+    ts("b0", T.b0[:], T.pi[:], 15, None, ALU.bitwise_and, None, "pi")
+    ts("b1", T.b1[:], T.pi[:], 1, None, ALU.bitwise_and, None)
+    ts("b2", T.b2[:], T.pi[:], 4, 1, ALU.logical_shift_right, ALU.bitwise_and)
+    copy("sf", T.sf[:], T.b0[:], "b0")
+    tt("e1", T.e1[:], T.b1[:], T.b2[:], ALU.is_equal, "b1", "b2")
+    ts("k2", T.k2[:], T.c2[:, 0:2], T.sf[:], float(KB - 1), ALU.add, ALU.min, "sf", "c2")
+    ts("k3", T.k3[:], T.c2[:, 0:2], T.sf[:], float(KH - 1), ALU.add, ALU.min)
+    ts("e2", T.e2[:], T.e1[:], float(C + 16), 16.0, ALU.mult, ALU.add, "e1")
+    ts("e3", T.e3[:], T.e1[:], float(H + 16), 16.0, ALU.mult, ALU.add)
+    copy("kl", T.kl[:], T.i24[:], "i24")
+    ts("tl", T.tl[:], T.k2[:], 16.0, T.e2[:], ALU.mult, ALU.add, "k2", "e2")
+    ts("tl2", T.tl2[:], T.k3[:], 16.0, T.e3[:], ALU.mult, ALU.add, "k3", "e3")
+    ts("mine", T.mine[:], T.c2[:], T.sf[:], float(S * rank - H * hl), ALU.add, ALU.add)
+    ts("mask", T.mask[:], T.mi[:], T.sf[:], None, ALU.is_gt, None, "mi")
 
     def sixteen(q, p, tok):
-        a = op("v", lambda: V.tensor_copy(T[p + "c"][:].bitcast(dt.uint32), T[q + "c"][:].bitcast(dt.uint32).indirect(T.pick[:])), tok, pick)
-        b = take("a", T[p + "s"][:], T[q + "s"][:], T.pick[:], tok, pick)
-        return a, b
+        copy(p + "c", T[p + "c"][:].bitcast(dt.uint32), T[q + "c"][:].bitcast(dt.uint32).indirect(T.pick[:]), tok, "pick")
+        take("a", p + "s", T[p + "s"][:], T[q + "s"][:], T.pick[:], tok, "pick")
+        return p + "c", p + "s"
 
-    def sorter(t, hf, mask):
-        row, trf, thr, sg, acc, pl = T["row" + t], T["trf" + t], T["thr" + t], T["sg" + t], T["acc" + t], T["pl" + t]
-        cmp_, sm, od, trb, later, init = T["cmp" + t], T["sum" + t], T["ord" + t], T["trb" + t], T["later" + t], T["init" + t]
-        lo = KH - (AL if hf else AE)
-        st = {}
+    def sorter(t, hf, arrive_v, arrive_a):
+        row, trf, thr, sg, acc, pl, plf = T["row" + t], T["trf" + t], T["thr" + t], T["sg" + t], T["acc" + t], T["pl" + t], T["plf" + t]
+        cmp_, sm, od, later = T["cmp" + t], T["sum" + t], T["ord" + t], T["later" + t]
+        hs = 1 - hf
+        ae, al, pos = PAR["ae" + t], PAR["al" + t], PAR["pos" + t]
+        lo = KH - (al if hf else ae)
+        hi = lo + ae + al
+        last = {}
+
+        def nm(*a):
+            return t + "".join(str(x) + "." for x in a)
+
+        def scores(h, a, b):
+            return row[:, 16 + H * h + a:16 + H * h + b]
 
         def of_half(h, scalar):
-            return [k for k in range(KH * h, KH * h + KH) if (lo <= k < lo + KA) == scalar]
-
-        def slot(k):
-            return k if k < lo else k - KA
+            return [k for k in range(KH * h, KH * h + KH) if (lo <= k < hi) == scalar]
 
         def own(k):
             c = 16 * (k // KH) + k % KH
             return thr[:, c:c + 1]
 
-        def scores(w, x, h, banks, *after):
-            pa = mm(banks[0], w, 0, x, H * h, H * h + H, *after)
-            pv = mm(banks[1], w, 0, x, H * h, H * h + H)
-            before = [st["t1"]] if "t1" in st else pads[t]
-            r = op("a", lambda: A.activation(row[:, 16 + H * h:16 + H * h + H], T["ps%d" % banks[0]][:, 0:H], ACT.Copy), pa, *before)
-            st["pv"], st["r", h] = pv, r
-            st["banks"] = banks
-
         def owns(h):
-            t2 = op("v", lambda: V.transpose(trf[:, TW * h + H + 32:TW * h + TW], T["ps%d" % st["banks"][1]][:, 0:H]), st["pv"])
-            st["t1"] = op("v", lambda: V.transpose(trf[:, TW * h:TW * h + H + 32], row[:, H * h:H * h + H + 32]), st["r", h])
-            st["th", h] = take("v", thr[:, 16 * h:16 * h + 16], trf[:, TW * h:TW * h + TW], T.tl2[:, 0:1], tl2, st["t1"], t2)
+            bank = T["ps%d" % (5 if h == hf else 3)]
+            turn(nm("t2", h), trf[:, TW * h + H + 32:TW * h + TW], bank[:, 0:H], nm("pv", h))
+            turn(nm("t1", h), trf[:, TW * h:TW * h + H + 32], row[:, H * h:H * h + H + 32], nm("r", h))
+
+        def thresholds(h):
+            take("v", nm("th", h), thr[:, 16 * h:16 * h + 16], trf[:, TW * h:TW * h + TW], T.tl2[:, 0:1], "tl2", nm("t1", h), nm("t2", h))
 
         def compare(k, a, b, *after):
-            n, c = 16 * k + 16, C * slot(k)
-            for x, y, how in ((a, min(b, n), ALU.is_ge), (max(a, n), b, ALU.is_gt)):
+            n, c = 16 * k + 16, C * k
+            for x, y, how in ((a, min(b, n), ALU.is_lt), (max(a, n), b, ALU.is_le)):
                 if x < y:
-                    st["cm", k] = ts(cmp_[:, c + x:c + y], row[:, 16 + x:16 + y], own(k), None, how, None, st["th", k // KH], *after)
-
-        def ties(h, fill):
-            a, b = H * h, H * h + H
-            same = op("v", lambda: V.tensor_tensor(T["same" + t][:, a:b], thr[:, 16 * h:16 * h + 16].indirect(T.kl[:, 0:KH]), row[:, 16 + a:16 + b], ALU.is_equal),
-                      st["th", h], kl)
-            fill[0]()
-            lt = op("v", lambda: V.tensor_tensor_scan(later[:, a:b], T["same" + t][:, a:b], T.mask[:, a:b], 0.0, ALU.add, ALU.mult), same, mask)
-            fill[1]()
-            ks = of_half(h, True)
-            st["wa", h] = op("v", lambda: V.tensor_tensor(sg[:, SGW * (ks[0] - lo) + C:SGW * (ks[-1] - lo + 1):SGW], later[:, 16 * ks[0] + 15:16 * ks[-1] + 16:16],
-                                                          T.k15[:, ks[0]:ks[-1] + 1], ALU.subtract), lt, k15)
-            ks = of_half(h, False)
-            st["wd", h] = ts(init[:, slot(ks[0]):slot(ks[-1]) + 1], later[:, 16 * ks[0] + 15:16 * ks[-1] + 16:16], -1.0, -1.0 - H, ALU.mult, ALU.add)
+                    last["cm", k] = ts(nm("cm", k, x), cmp_[:, c + x:c + y], row[:, 16 + x:16 + y], own(k), -0.5, how, ALU.add, nm("th", k // KH), *after)
 
         def total(k):
-            c = slot(k)
-            st["sum", k] = op("v", lambda: V.tensor_tensor_scan(sm[:, H * c:H * c + H], cmp_[:, C * c:C * c + H], cmp_[:, C * c + H:C * c + C],
-                                                                init[:, c:c + 1], ALU.add, ALU.add), st["cm", k], st["wd", k // KH])
+            scan(nm("sum", k), sm[:, H * k:H * k + H], cmp_[:, C * k:C * k + H], cmp_[:, C * k + H:C * k + C],
+                 later[:, 16 * k + 15:16 * k + 16], ALU.add, ALU.add, last["cm", k], nm("lt", k // KH))
+
+        def same(h):
+            tt(nm("same", h), T["same" + t][:, H * h:H * h + H], thr[:, 16 * h:16 * h + 16].indirect(T.kl[:, 0:KH]), scores(h, 0, H), ALU.is_equal, nm("th", h), "kl")
+
+        def behind(h):
+            scan(nm("lt", h), later[:, H * h:H * h + H], T["same" + t][:, H * h:H * h + H], T.mask[:], 0.0, ALU.add, ALU.mult, nm("same", h), "mask")
+
+        def for_scalar(h):
+            ks = of_half(h, True)
+            tt(nm("wa", h), sg[:, SGW * ks[0] + C:SGW * (ks[-1] + 1):SGW], later[:, 16 * ks[0] + 15:16 * ks[-1] + 16:16], T.k15[:, ks[0]:ks[-1] + 1],
+               ALU.subtract, nm("lt", h), "k15")
 
         def sign(k, a, b, *after):
-            c = SGW * (k - lo)
-            st["sn", k] = op("a", lambda: A.activation(sg[:, c + a:c + b], row[:, 16 + a:16 + b], ACT.Sign, bias=own(k), scale=-1.0), st["th", k // KH], *after)
+            c = SGW * k
+            last["sn", k] = act(nm("sn", k, a, b), sg[:, c + a:c + b], row[:, 16 + a:16 + b], ACT.Sign, nm("th", k // KH), *after, bias=own(k), scale=-1.0)
 
         def smaller(k):
-            i, n = k - lo, 16 * k + 16
-            v = sg[:, SGW * i:SGW * i + n]
-            st["done", k] = op("a", lambda: A.activation(v, v, ACT.Relu, accum_out=acc[:, i:i + 1]), st["sn", k])
+            v = sg[:, SGW * k:SGW * k + 16 * k + 16]
+            last["done", k] = act(nm("sm", k), v, v, ACT.Relu, last["sn", k], accum_out=acc[:, k:k + 1])
 
         def larger(k):
-            i, n = k - lo, 16 * k + 16
-            v = sg[:, SGW * i + n:SGW * i + C + 1]
-            st["done", k] = op("a", lambda: A.activation(v, v, ACT.Relu, scale=-1.0, accum_out=acc[:, KA + i:KA + i + 1]), st["sn", k], st["wa", k // KH])
+            v = sg[:, SGW * k + 16 * k + 16:SGW * k + C + 1]
+            last["done", k] = act(nm("lg", k), v, v, ACT.Relu, last["sn", k], nm("wa", k // KH), scale=-1.0, accum_out=acc[:, KB + k:KB + k + 1])
 
-        a1, z1, a2, z2 = H * hf, H * hf + H, H * (1 - hf), H * (1 - hf) + H
+        def places_v(ks):
+            return ts(nm("p0", ks[0]), pl[:, ks[0]:ks[-1] + 1], sm[:, H * ks[0] + H - 1:H * ks[-1] + H:H], -1.0, H - 1.0, ALU.mult, ALU.add, nm("sum", ks[-1]))
 
-        def first_vector(ks):
-            for k in ks:
-                compare(k, a1, z1)
+        def diff_a(ks):
+            a, b = ks[0], ks[-1] + 1
+            return tt(nm("d", a), plf[:, a:b], acc[:, KB + a:KB + b], acc[:, a:b], ALU.subtract, *[last["done", k] for k in ks])
 
-        def first():
-            owns(hf)
-            ks = of_half(hf, False)
-            ties(hf, [lambda: compare(ks[0], a1, z1), lambda: compare(ks[1], a1, z1)])
-            ka = of_half(hf, True)
-            for k in ka:
-                sign(k, a1, z1)
-            for k in ka:
+        def places_a(ks):
+            a, b = ks[0], ks[-1] + 1
+            return copy(nm("p1", a), pl[:, a:b], plf[:, a:b], nm("d", a))
+
+        def place_a(k):
+            return ts(nm("p2", k), pl[:, k:k + 1], acc[:, KB + k:KB + k + 1], acc[:, k:k + 1], None, ALU.subtract, None, last["done", k])
+
+        def spread(a, b, *after):
+            return op("v", nm("sc", a), lambda: V.tensor_copy(od[:, 16:C + 16].indirect(pl[:, a:b]), T.num[:, 16 * a:16 * b]), "num", *after)
+
+        a1, z1, a2, z2 = H * hf, H * hf + H, H * hs, H * hs + H
+        r = nm("r", hs)
+
+        act(nm("r", hf), scores(hf, 0, H), T.ps4[:, 0:H], ACT.Copy, nm("pa", hf), "padA" + t, "padB" + t, "padC" + t)
+        ka, kb = of_half(hf, True), of_half(hs, True)
+        e0 = PAR["e0" + t]
+        for k in ka[:e0]:
+            sign(k, a1, z1)
+        if t == "2":
+            for k in ka[:PAR["ea"]]:
                 (larger if hf else smaller)(k)
-            return ks[2:]
-
-        def places(h):
-            ka, kv = of_half(h, True), of_half(h, False)
-            a, b = ka[0] - lo, ka[-1] - lo + 1
-            d = op("v", lambda: V.tensor_tensor(T["plf" + t][:, a:b], acc[:, KA + a:KA + b], acc[:, a:b], ALU.subtract), st["done", ka[0]], st["done", ka[-1]])
-            p0 = ts(pl[:, kv[0]:kv[-1] + 1], sm[:, H * slot(kv[0]) + H - 1:H * slot(kv[-1]) + H:H], float(H), None, ALU.add, None, st["sum", kv[-1]])
-            p1 = op("v", lambda: V.tensor_copy(pl[:, ka[0]:ka[-1] + 1], T["plf" + t][:, a:b]), d)
-            before = [st["sc"]] if "sc" in st else pads[t]
-            st["sc"] = op("v", lambda: V.tensor_copy(od[:, 16:C + 16].indirect(pl[:, KH * h:KH * h + KH]), T.num[:, H * h:H * h + H]), p0, p1, num, *before)
-            return p1
-
-        def second():
-            h = 1 - hf
-            r = st["r", h]
-            ke, kv = of_half(hf, False), of_half(h, False)
-            for k in of_half(hf, True):
-                sign(k, a2, z2, r)
-            owns(h)
-            ties(h, [lambda: compare(ke[0], a2, z2, r), lambda: compare(ke[1], a2, z2, r)])
-            for k in of_half(hf, True):
-                (smaller if hf else larger)(k)
-            ka = of_half(h, True)
-            for k in ka[:AHEAD]:
-                sign(k, 0, C)
-            for i, k in enumerate(ka):
-                if i + AHEAD < len(ka):
-                    sign(ka[i + AHEAD], 0, C)
+            arrive_a()
+            for k in ka[PAR["ea"]:e0]:
+                (larger if hf else smaller)(k)
+        act(r, scores(hs, 0, H), T.ps2[:, 0:H], ACT.Copy, nm("pa", hs), nm("t1", hf))
+        if t == "1":
+            for k in ka[:e0]:
                 smaller(k)
-                larger(k)
-            todo = ke[:2]
-            for k in ke[2:] + kv:
-                if k in ke:
-                    compare(k, a2, z2)
-                else:
-                    compare(k, 0, C)
-                total(todo.pop(0))
-                todo.append(k)
-            for k in todo:
-                total(k)
-            places(hf)
-            p = places(h)
-            u1 = op("v", lambda: V.transpose(trb[:, 0:C + 32], od[:]), st["sc"])
-            u2 = op("v", lambda: V.transpose(trb[:, C + 32:2 * C + 32], od[:, 16:C + 16]))
-            lists = {}
-            for b in (1, 3, 0, 2):
-                lists[b] = ts(T["l4" + t][:, 32 * b:32 * b + 32], trb[:].indirect(T.tl[:]), 4.0, 4.0 * H + b, ALU.mult, ALU.add, u1, u2, tl)
-            return lists, p, st["sc"]
+        for k in ka[:e0]:
+            sign(k, a2, z2, r)
+        whole = ka[e0:] + (kb if hf else kb[::-1])
+        sign(whole[0], 0, C, r)
+        for k in ka[:e0]:
+            (smaller if hf else larger)(k)
+        for i, k in enumerate(whole):
+            if i + 1 < len(whole):
+                sign(whole[i + 1], 0, C)
+            smaller(k)
+            larger(k)
 
-        return scores, first, first_vector, second
+        ke, kv = of_half(hf, False), of_half(hs, False)
+        owns(hf)
+        thresholds(hf)
+        if pos < 0:
+            arrive_v()
+        same(hf)
+        compare(ke[0], a1, z1)
+        behind(hf)
+        compare(ke[1], a1, z1)
+        for_scalar(hf)
+        v0 = PAR["v0" + t]
+        for i, k in enumerate(ke[2:v0]):
+            if i == pos:
+                arrive_v()
+            compare(k, a1, z1)
+        if pos >= v0 - 2:
+            arrive_v()
+        owns(hs)
+        compare(ke[0], a2, z2, r)
+        thresholds(hs)
+        compare(ke[1], a2, z2)
+        same(hs)
+        total(ke[0])
+        behind(hs)
+        total(ke[1])
+        for_scalar(hs)
+        prev = None
+        for k in ke[2:] + kv:
+            if k in ke[:v0]:
+                compare(k, a2, z2)
+            else:
+                compare(k, 0, C)
+            if prev is not None:
+                total(prev)
+            prev = k
+            if k == kv[PAR["sa" + t]]:
+                diff_a(ka)
+                p0 = places_v(ke)
+                p1 = places_a(ka)
+        s0 = spread(KH * hf, KH * hf + KH, p0, p1, "padD" + t, "padE" + t)
+        total(prev)
+        nl = PAR["nl" + t]
+        tail = kb[-nl:] if hf else kb[:nl]
+        head = [k for k in kb if k not in tail]
+        diff_a(head)
+        p0 = places_v(kv)
+        p1 = places_a(head)
+        rest = sorted(head + kv)
+        s1 = spread(rest[0], rest[-1] + 1, s0, p0, p1)
+        return spread(tail[0], tail[-1] + 1, s1, *[place_a(k) for k in whole[-nl:]])
 
     def write_order(t, out, tok):
-        f = op("a", lambda: A.activation(T["of" + t][:], T["ord" + t][:, 16:C + 16], ACT.Identity, bias=float(H)), tok)
+        act("of" + t, T["of" + t][:], T["ord" + t][:, 16:C + 16], ACT.Identity, tok, bias=float(H))
         for k in range(8):
-            dma("s", "st", out[k:k + 1, :], T["of" + t][16 * k:16 * k + 1, :], f)
+            dma("s", "st", "so%s%d" % (t, k), out[k:k + 1, :], T["of" + t][16 * k:16 * k + 1, :], "of" + t)
+
+    def score_mm(t, w, x, h, first, *after):
+        mm(t + "pa.%d." % h, 4 if first else 2, w, 0, x, H * h, H * h + H, *after)
+        mm(t + "pv.%d." % h, 5 if first else 3, w, 0, x, H * h, H * h + H)
 
     mine, pairs = plan_of(rank, T, topo)
     off = topo.engines(core, T.cores[mine[0]])
-    cnt["sent"] = 0
 
-    def leave_early(stage, tok):
+    def remote(name, tr, *after):
+        todo["p"].append((name, None, 0, lambda: g.remote_dma_fused(tr, local_sem=T.sem.sent), after))
+
+    def far(stage, tok):
         src, rel, dst, t = STAGES[stage]
-        wait("p", [tok])
         for kind in "cs":
             tr = []
             for i, (c, ds) in enumerate(pairs):
-                eng = topo.engines(core, c)
-                eng = eng[8 * i:8 * i + 8] if kind == "c" else [e for e in eng if e not in off][4 * i:4 * i + 4]
+                eng = relay_engines(t, kind, i, topo.engines(core, c), off)
                 tr.append(transfer(topo, core, c, eng, T.sem["h" + kind + t],
                                    cols(T, src, kind, S * ds[0], S * ds[0] + 2 * S), cols(T, rel, kind, 0, 2 * S)))
                 cnt["sent"] += len(eng)
-            g.remote_dma_fused(tr, local_sem=T.sem.sent)
-        cnt["far" + t] = 2 * 4 * 4
-        return ("far" + t, cnt["far" + t])
+            remote("rel" + kind + t, tr, tok)
 
-    def leave_late(stage, tok):
+    def near(stage, tok):
         src, rel, dst, t = STAGES[stage]
-        wait("p", [tok])
         deal = {"c": (off[0:4], off[4:6], off[6:8]), "s": (off[0:2], off[2:4], off[4:8])}
         for kind in "cs":
             tr = []
             for d, eng in zip(mine, deal[kind]):
                 tr.append(transfer(topo, core, T.cores[d], eng, T.sem["near" + t],
                                    cols(T, src, kind, S * d, S * d + S), cols(T, dst, kind, S * rank, S * rank + S)))
-            g.remote_dma_fused(tr, local_sem=T.sem.sent)
             cnt["sent"] += 8
-        for kind in "cs":
-            own = dma("s", "own" + t, cols(T, dst, kind, S * rank, S * rank + S), cols(T, src, kind, S * rank, S * rank + S), tok)
-        cnt["near" + t] = 16
-        return own, ("near" + t, 16)
+            remote("near" + kind + t, tr, tok)
 
-    qu = quant("uq", T.us, 0, 128, lu)
-    up = sixteen("uq", "up", qu)
-    mask = ts(T.mask[:], T.mi[:], T.sf[:], None, ALU.is_gt, None, mi, sf)
-    scores, first, first_vector, second = sorter("1", 0, mask)
-    scores("up", "xq", 0, (0, 1), quant("xq", T.xs, 0, H, lxa), *up)
-    left = first()
-    scores("up", "xq", 1, (2, 3), quant("xq", T.xs, H, C, lxb))
-    first_vector(left)
-    lists, pl1, ord1 = second()
+    def keep(stage, tok):
+        src, rel, dst, t = STAGES[stage]
+        a, b = S * rank, S * rank + S
+        copy("ownc" + t, T[dst + "c"][:, a:b].bitcast(dt.uint32), T[src + "c"][:, H * hl:H * hl + H].bitcast(dt.uint32).indirect(T.mine[:, 0:3]), tok, "mine")
+        return take("v", "owns" + t, T[dst + "s"][:, a:b], T[src + "s"][:, H * hl:H * hl + H], T.mine[:, 0:3], tok)
 
-    def part(q, b, h):
-        a = 32 * b + KH * h
-        return take(q, T.ft[:, 4 * H * h + b:4 * H * (h + 1):4], T.xs[:], T.l41[:, a:a + KH], lists[b], lxa, lxb)
+    def moved(name, b):
+        return T[name + "1"][:, 16:15 + 4 * C] if b % 2 else T[name][:]
 
-    got = [part("a", 1, he), part("a", 3, he), part("v", 0, he), part("v", 2, he)]
-    early = leave_early(0, quant("fq", T.ft, H * he, H * he + H, *got))
-    got = [part("a", 1, hl), part("a", 3, hl), part("v", 0, hl), part("a", 2, hl)]
-    qf = quant("fq", T.ft, H * hl, H * hl + H, *got)
-    late = leave_late(0, qf)
+    def send(stage, name, tile, h, mark, key, steps):
+        got = [mark + "%s.%d" % (e[1], H * h + SPAN[e[2]][0]) for e in steps.split() if e[0] == key]
+        (near if h == hl else far)(stage, quant(name + str(h), STAGES[stage][0], tile, H * h, H * h + H, *got))
 
-    qv = quant("vq", T.vs, 0, 128, lv)
-    pads["2"] = margins("2")
-    half = op("v", lambda: V.memset(T.half[:], 0.5))
-    vp = sixteen("vq", "vp", qv)
-    write_order("1", T.oa, ord1)
-    ze = op("v", lambda: V.memset(T.et[:], 0.0))
+    quant("qu", "uq", T.us, 0, 128, "lu")
+    up = sixteen("uq", "up", "qu")
+    quant("qx0", "xq", T.xs, 0, H, "lxa")
+    score_mm("1", "up", "xq", 0, True, "qx0", *up)
+    score_mm("1", "up", "xq", 1, False, "qx1")
+    ord1 = sorter("1", 0, lambda: quant("qx1", "xq", T.xs, H, C, "lxb"), lambda: None)
 
-    def layer(h, banks, *after):
-        rs = [mm(banks[b], "wq", 128 * b, "aq", H * h, H * h + H, lw, qf, *after) for b in (1, 0, 3, 2)]
-        got = []
-        for b, tok in zip((1, 0, 3, 2), rs):
-            out, ps = T.ht[:, 4 * H * h + b:4 * H * (h + 1):4], T["ps%d" % banks[b]][:, 0:H]
-            if b % 2:
-                got.append(op("a", lambda: A.activation(out, ps, ACT.Copy, scale=0.00390625), tok))
+    for q in "av":
+        for c in PAR["f" + q].split():
+            h = he if c[0] in "yULM" or c == "q1" else hl
+            if c[0] in "uU":
+                turn("u1%d" % h, T.trb1[:, TW * h:TW * h + H + 32], T.ord1[:, H * h:H * h + H + 32], ord1)
+                turn("u2%d" % h, T.trb1[:, TW * h + H + 32:TW * h + TW], T.ord1[:, 16 + H * h:16 + H * h + H])
+            elif c[0] in "lL":
+                ts("l0%d" % h, T.l41[:, 16 * h:16 * h + 16], T.trb1[:, TW * h:TW * h + TW].indirect(T.tl2[:, 0:1]), 4.0, 4.0 * H, ALU.mult, ALU.add, "u2%d" % h)
+            elif c[0] in "mM":
+                ts("l1%d" % h, T.l41[:, 32 + 16 * h:48 + 16 * h], T.l41[:, 16 * h:16 * h + 16], 2.0, None, ALU.add, None, "l0%d" % h)
+            elif c == "o":
+                write_order("1", T.oa, ord1)
+            elif c[0] == "q":
+                send(0, "qf", T.ft, h, "f", "xy"[int(c[1])], PAR["fa"] + " " + PAR["fv"])
             else:
-                got.append(ts(out, ps, 0.00390625, None, ALU.mult, None, tok))
-        return quant("hq", T.ht, H * h, H * h + H, *got)
+                b, (x, y) = int(c[1]), SPAN[c[2]]
+                a = 32 * (b // 2) + 16 * h
+                take(q, "f%d.%d" % (b, H * h + x), T.ft[:, 4 * (H * h + x) + b:4 * (H * h + y):4], moved("xs", b), T.l41[:, a + x // 16:a + y // 16],
+                     "l%d%d" % (b // 2, h), "lxa", "lxb", "lx1")
+    own1 = keep(0, "qf%d" % hl)
 
-    scores, first, first_vector, second = sorter("2", hl, mask)
-    qe = layer(hl, (0, 1, 2, 3), *late)
-    scores("vp", "hq", hl, (4, 5), qe, *vp)
-    left = first()
-    first_vector(left[:-2])
-    qh = layer(he, (6, 7, 0, 1), qe, early)
-    scores("vp", "hq", he, (2, 3), qh)
-    first_vector(left[-2:])
-    lists, pl2, ord2 = second()
+    quant("qv", "vq", T.vs, 0, 128, "lv")
+    margins("2")
+    vp = sixteen("vq", "vp", "qv")
 
-    def fwd(q, b):
-        return take(q, T.hs[:, C * b:C * b + C], T.ht[:], T.l42[:, 32 * b:32 * b + KB], lists[b], qh)
+    def layer_mm(h, banks, *after):
+        for b in (1, 0, 3, 2):
+            mm("r%d%d" % (b, h), banks[b], "wq", 128 * b, "aq", H * h, H * h + H, "lw", *after)
 
-    def scan(b, tok):
-        return op("v", lambda: V.tensor_tensor_scan(T.ss[:, C * b:C * b + C], T.half[:], T.hs[:, C * b:C * b + C], 0.0, ALU.mult, ALU.max), tok, half)
+    def layer(q, h, banks, bs):
+        for b in bs:
+            out, ps = T.ht[:, 4 * H * h + b:4 * H * (h + 1):4], T["ps%d" % banks[b]][:, 0:H]
+            if q == "a":
+                act("h%d%d" % (b, h), out, ps, ACT.Copy, "r%d%d" % (b, h), scale=0.00390625)
+            else:
+                ts("h%d%d" % (b, h), out, ps, 0.00390625, None, ALU.mult, None, "r%d%d" % (b, h))
 
-    def back(q, out, src, pl, b, h, *after):
-        return take(q, out[:, 4 * H * h + b:4 * H * (h + 1):4], src[:, C * b:C * b + C], pl[:, KH * h:KH * h + KH], *after)
+    def quant_h(h):
+        quant("qh%d" % h, "hq", T.ht, H * h, H * h + H, *["h%d%d" % (b, h) for b in range(4)])
 
-    f1 = fwd("a", 1)
-    f3 = fwd("a", 3)
-    f0 = fwd("v", 0)
-    s1 = scan(1, f1)
-    s0 = scan(0, f0)
-    s3 = scan(3, f3)
-    f2 = fwd("v", 2)
-    s2 = scan(2, f2)
-    sc = (s0, s1, s2, s3)
-    got = [back(q, T.tt, T.ss, T.pl2, b, he, sc[b], pl2) for q, b in (("a", 1), ("a", 0), ("a", 3), ("v", 2))]
-    early = leave_early(1, quant("tq", T.tt, H * he, H * he + H, *got))
-    got = [back(q, T.tt, T.ss, T.pl2, b, hl, sc[b]) for q, b in (("a", 1), ("a", 0), ("a", 3), ("v", 2))]
-    qt = quant("tq", T.tt, H * hl, H * hl + H, *got)
-    late = leave_late(1, qt)
+    layer_mm(hl, (0, 1, 2, 3), own1, "near1", "qf0", "qf1")
+    layer("a", hl, (0, 1, 2, 3), (1, 3))
+    layer("v", hl, (0, 1, 2, 3), (0, 2))
+    quant_h(hl)
+    score_mm("2", "vp", "hq", hl, True, "qh%d" % hl, *vp)
+    layer_mm(he, (6, 7, 0, 1), "far1")
+    score_mm("2", "vp", "hq", he, False, "qh%d" % he)
+    dma("s", "lh", "lh1", T.ht1[:, 15:15 + 4 * C], T.ht[:], "qh0", "qh1")
+    on_a = (1, 0, 3, 2)[:PAR["la2"]]
 
-    ones = [ts(T.et[:, 512 * b + b:512 * b + 512:4], T.idn[:], 0.0, None, ALU.is_equal, None, ze, idn) for b in range(4)]
-    qe = quant("eq4", T.et, 0, 512, *ones)
-    qm = quant("mq", T.ms, 0, 128, lm)
+    def arrive_v():
+        layer("v", he, (6, 7, 0, 1), [b for b in (1, 0, 3, 2) if b not in on_a])
+        quant_h(he)
+
+    ord2 = sorter("2", hl, arrive_v, lambda: layer("a", he, (6, 7, 0, 1), on_a))
+    turn("w1", T.trb2[:, 0:C + 32], T.ord2[:], ord2)
+    turn("w2", T.trb2[:, C + 32:2 * C + 32], T.ord2[:, 16:C + 16])
+    ts("m0", T.l42[:, 0:32], T.trb2[:, 0:2 * C + 32].indirect(T.tl[:]), 4.0, 4.0 * H, ALU.mult, ALU.add, "w2", "tl")
     write_order("2", T.ob, ord2)
 
-    def add(h, bank, *after):
-        ds = [mm(bank + b, "eq4", 128 * b, "bq", H * h, H * h + H, qe, qt, *after) for b in range(4)]
-        return [op("v", lambda: V.tensor_tensor(T.zs[:, C * b + H * h:C * b + H * h + H], T["ps%d" % (bank + b)][:, 0:H],
-                                                T.ft[:, 4 * H * h + b:4 * H * (h + 1):4], ALU.add), ds[b]) for b in range(4)]
+    def back(q, name, out, src, pl, b, a, z, *after):
+        return take(q, name + "%d.%d" % (b, a), out[:, 4 * a + b:4 * z:4], src[:, C * b:C * b + C], pl[:, a // 16:z // 16], *after)
 
-    add(hl, 4, *late)
-    sums = add(he, 0, early)
+    ts("m1", T.l42[:, 32:32 + KB], T.l42[:, 0:KB], 2.0, None, ALU.add, None, "m0")
+    for q in "av":
+        for c in PAR["s" + q].split():
+            b = int(c[1])
+            h = hl if c[0] == "y" or c == "q1" else he
+            if c[0] == "f":
+                take(q, "fw%d" % b, T.hs[:, C * b:C * b + C], moved("ht", b), T.l42[:, 32 * (b // 2):32 * (b // 2) + KB], "m%d" % (b // 2), "lh1")
+            elif c[0] == "s":
+                scan("s%d" % b, T.ss[:, C * b:C * b + C], T.half[:], T.hs[:, C * b:C * b + C], 0.0, ALU.mult, ALU.max, "fw%d" % b, "half")
+            elif c[0] == "q":
+                send(1, "qt", T.tt, h, "t", "xy"[b], PAR["sa"] + " " + PAR["sv"])
+            else:
+                x, y = SPAN[c[2]]
+                back(q, "t", T.tt, T.ss, T.pl2, b, H * h + x, H * h + y, "s%d" % b)
+    own2 = keep(1, "qt%d" % hl)
 
-    def home(q, b, h):
-        return back(q, T.zt, T.zs, T.pl1, b, h, sums[b], pl1)
+    quant("qe", "eq4", T.et, 0, 512, "et")
+    quant("qm", "mq", T.ms, 0, 128, "lm")
 
-    one = [home("a", 0, 0), home("a", 1, 0), home("a", 2, 0), home("v", 3, 0)]
-    two = [home("a", 0, 1), home("a", 1, 1), home("v", 3, 1)]
-    qz = quant("zq", T.zt, 0, H, *one)
-    y0 = mm(4, "mq", 0, "zq", 0, H, qz, qm)
-    dma("s", "st", T.oc[:, 0:4 * H], words(T.zqc[:, 0:H]), qz)
-    two.append(home("v", 2, 1))
-    c0 = op("a", lambda: A.activation(T.y0[:], T.ps4[:, 0:H], ACT.Copy), y0)
-    dma("s", "st", T.y[:, 0:H], T.y0[:], c0)
-    qz = quant("zq", T.zt, H, C, *two)
-    y1 = mm(5, "mq", 0, "zq", H, C, qz)
-    dma("s", "st", T.oc[:, 4 * H:4 * C], words(T.zqc[:, H:C]), qz)
-    c1 = op("v", lambda: V.tensor_copy(T.y1[:], T.ps5[:, 0:H]), y1)
-    for k in range(4):
-        q = "sa"[k // 2]
-        dma(q, "st" if q == "s" else "sta", T.osc[4 * k:4 * k + 4, :], T.zqs[32 * k:32 * k + 4, :], qz)
-    dma("a", "sta", T.y[:, H:C], T.y1[:], c1)
+    def add(b, h):
+        bank = (4 if h == hl else 0) + b
+        mm("d%d%d" % (b, h), bank, "eq4", 128 * b, "bq", H * h, H * h + H, "qe", "qt0", "qt1", *((own2, "near2") if h == hl else ("far2",)))
+        tt("z%d%d" % (b, h), T.zs[:, C * b + H * h:C * b + H * h + H], T["ps%d" % bank][:, 0:H], T.ft[:, 4 * H * h + b:4 * H * (h + 1):4], ALU.add, "d%d%d" % (b, h))
 
-    wait("p", [(s, cnt[s]) for s in cnt])
+    def step(q, c):
+        i = int(c[1])
+        a, z = H * i, H * i + H
+        st = "st" if q == "s" else "sta"
+        if c[0] == "q":
+            quant("qz%d" % i, "zq", T.zt, a, z, *["o%d.%d" % (b, a) for b in range(4)])
+            mm("y%d" % i, 4 + i, "mq", 0, "zq", a, z, "qz%d" % i, "qm")
+        elif c[0] == "y":
+            if q == "a":
+                act("c%d" % i, T["y%d" % i][:], T["ps%d" % (4 + i)][:, 0:H], ACT.Copy, "y%d" % i)
+            else:
+                copy("c%d" % i, T["y%d" % i][:], T["ps%d" % (4 + i)][:, 0:H], "y%d" % i)
+        elif c[0] == "C":
+            dma(q, st, "sc%d" % i, T.oc[:, 4 * a:4 * z], words(T.zqc[:, a:z]), "qz%d" % i)
+        elif c[0] == "Y":
+            dma(q, st, "sy%d" % i, T.y[:, a:z], T["y%d" % i][:], "c%d" % i)
+        elif c[0] == "S":
+            dma(q, st, "ss%d" % i, T.osc[4 * i:4 * i + 4, :], T.zqs[32 * i:32 * i + 4, :], "qz1")
+        else:
+            back(q, "o", T.zt, T.zs, T.pl1, int(c[0]), a, z, "z%s0" % c[0], "z%s1" % c[0])
+
+    for c in PAR["adds"].split():
+        add(int(c[1]), hl if c[0] == "l" else he)
+    for q in "avs":
+        for c in PAR["h" + q].split():
+            step(q, c)
+
+    issue()
+    wait("p", [(s, cnt[s]) for s in cnt] + [done[s] for s in ("near1", "near2", "far1", "far2")])

@@ -7,7 +7,7 @@ KB = C // 16
 KH = KB // 2
 TW = 2 * H + 32
 SGW = C + 8
-PAR = {"ae1": 5, "al1": 6, "ae2": 5, "al2": 6, "e01": 2, "e02": 5, "ea": 3, "v01": 3, "v02": 7, "pos1": -1, "pos2": 3, "la2": 2,
+PAR = {"ae1": 5, "al1": 6, "ae2": 5, "al2": 6, "e01": 2, "e02": 5, "ea": 2, "v01": 3, "v02": 7, "pos1": -1, "pos2": 3, "la2": 2,
        "sa1": 2, "sa2": 2, "nl1": 2, "nl2": 2,
        "fa": "x1w x3w y1w y3w y2a o", "fv": "u l U m x0w L x2w M q0 y0w y2b q1",
        "sa": "f1w f3w x1w x0w x3w y1w y0w y3a", "sv": "f0w s1 s0 f2w s3 s2 x2w q0 y2w y3b q1",
@@ -23,19 +23,19 @@ def _sb(name, cols, dtype):
 
 
 for _n, _c in (("xs", 4 * C), ("us", 512), ("vs", 512), ("ms", 512), ("ft", 4 * C), ("ht", 4 * C), ("hs", 4 * C), ("ss", 4 * C),
-               ("tt", 4 * C), ("zs", 4 * C), ("zt", 4 * C), ("et", 2048), ("eo", 2048), ("mi", H), ("mask", H), ("num", C), ("half", C),
-               ("xs1", 4 * C + 16), ("ht1", 4 * C + 16)):
+               ("tt", 4 * C), ("zs", 4 * C), ("zt", 4 * C), ("et", 2048), ("eo", 2048), ("mi", H), ("mask", H), ("one", H), ("keep", H),
+               ("num", C), ("half", C), ("xs1", 4 * C + 16), ("ht1", 4 * C + 16)):
     _sb(_n, _c, BF)
 for _n, _c in (("xq", C), ("uq", 128), ("up", 128), ("vq", 128), ("vp", 128), ("mq", 128), ("wq", 512), ("eq4", 512), ("fq", C),
                ("aq", C), ("hq", C), ("tq", C), ("bq", C), ("zq", C), ("r1", 2 * S), ("r2", 2 * S)):
     _sb(_n + "c", _c, CODE)
     _sb(_n + "s", _c, PLANE)
 for _t in "12":
-    for _n, _c, _d in (("row", C + 32, F32), ("trf", 2 * TW, F32), ("thr", 32, F32), ("same", C, BF), ("later", C, BF),
+    for _n, _c, _d in (("lone", C, F32), ("thr", C, F32), ("same", C, BF), ("later", C, BF),
                        ("cmp", KB * C, BF), ("sum", KB * H, BF), ("sg", KB * SGW, F32), ("acc", 2 * KB, F32), ("plf", KB, F32), ("pl", KB, U16),
                        ("ord", C + 32, BF), ("trb", 2 * TW, BF), ("l4", 64, U16), ("of", C, F32)):
         _sb(_n + _t, _c, _d)
-for _n, _c, _d in (("i8", 8, I32), ("pick", 8, U16), ("i24", KB, I32), ("kl", KB, U16), ("pi", 1, I32), ("b0", 1, I32), ("b1", 1, I32),
+for _n, _c, _d in (("i8", 8, I32), ("pick", 8, U16), ("pi", 1, I32), ("b0", 1, I32), ("b1", 1, I32),
                    ("b2", 1, I32), ("sf", 1, F32), ("e1", 1, F32), ("e2", 1, F32), ("c2", 4, F32), ("k2", 2, F32), ("tl", 2, U16),
                    ("k15", KB, F32), ("e3", 1, F32), ("k3", 2, F32), ("tl2", 2, U16), ("mine", 4, U16), ("y0", H, F32), ("y1", H, F32)):
     _sb(_n, _c, _d)
@@ -209,19 +209,15 @@ def rank_program(g, core, T, topo):
 
     iota("i8", [[16, 8]], 0, 0, True)
     iota("pi", [[1, 1]], 0, 1, True)
-    iota("c2", [[16, 4]], 0, 0, False)
-    iota("i24", [[1, KB]], 0, 0, True)
-    iota("k15", [[16, KB]], 15, 0, False)
     iota("mi", [[0, KH], [1, 16]], 0, 0, False)
+    iota("c2", [[16, 4]], 0, 0, False)
+    iota("k15", [[16, KB]], 15, 0, False)
     iota("num", [[1, C]], -H, 0, False)
     op("p", "half", lambda: g.affine_select(T.half[:], T.num[:], [[0, C]], ALU.is_gt, 0.5, 0, 0), "num")
     iota("eo", [[0, 2048]], 1, 0, False)
     op("p", "et", lambda: g.affine_select(T.et[:], T.eo[:], [[-1, 4], [1, 512]], ALU.is_equal, 0.0, 0, -4), "eo")
 
     def margins(t):
-        fill("padA" + t, T["row" + t][:, 0:16], 0.0)
-        fill("padB" + t, T["row" + t][:, C + 16:C + 32], 0.0)
-        fill("padC" + t, T["row" + t][:, H:H + 32], 0.0)
         fill("padD" + t, T["ord" + t][:, 0:16], 0.0)
         fill("padE" + t, T["ord" + t][:, C + 16:C + 32], 0.0)
 
@@ -232,15 +228,16 @@ def rank_program(g, core, T, topo):
     ts("b2", T.b2[:], T.pi[:], 4, 1, ALU.logical_shift_right, ALU.bitwise_and)
     copy("sf", T.sf[:], T.b0[:], "b0")
     tt("e1", T.e1[:], T.b1[:], T.b2[:], ALU.is_equal, "b1", "b2")
-    ts("k2", T.k2[:], T.c2[:, 0:2], T.sf[:], float(KB - 1), ALU.add, ALU.min, "sf", "c2")
+    ts("keep", T.keep[:], T.mi[:], 1.0, None, ALU.min, None, "mi")
+    ts("one", T.one[:], T.mi[:], T.sf[:], None, ALU.is_equal, None, "sf")
+    ts("mask", T.mask[:], T.mi[:], T.sf[:], None, ALU.is_gt, None)
+    ts("k2", T.k2[:], T.c2[:, 0:2], T.sf[:], float(KB - 1), ALU.add, ALU.min, "c2")
     ts("k3", T.k3[:], T.c2[:, 0:2], T.sf[:], float(KH - 1), ALU.add, ALU.min)
     ts("e2", T.e2[:], T.e1[:], float(C + 16), 16.0, ALU.mult, ALU.add, "e1")
     ts("e3", T.e3[:], T.e1[:], float(H + 16), 16.0, ALU.mult, ALU.add)
-    copy("kl", T.kl[:], T.i24[:], "i24")
+    ts("mine", T.mine[:], T.c2[:], T.sf[:], float(S * rank - H * hl), ALU.add, ALU.add)
     ts("tl", T.tl[:], T.k2[:], 16.0, T.e2[:], ALU.mult, ALU.add, "k2", "e2")
     ts("tl2", T.tl2[:], T.k3[:], 16.0, T.e3[:], ALU.mult, ALU.add, "k3", "e3")
-    ts("mine", T.mine[:], T.c2[:], T.sf[:], float(S * rank - H * hl), ALU.add, ALU.add)
-    ts("mask", T.mask[:], T.mi[:], T.sf[:], None, ALU.is_gt, None, "mi")
 
     def sixteen(q, p, tok):
         copy(p + "c", T[p + "c"][:].bitcast(dt.uint32), T[q + "c"][:].bitcast(dt.uint32).indirect(T.pick[:]), tok, "pick")
@@ -248,47 +245,51 @@ def rank_program(g, core, T, topo):
         return p + "c", p + "s"
 
     def sorter(t, hf, arrive_v, arrive_a):
-        row, trf, thr, sg, acc, pl, plf = T["row" + t], T["trf" + t], T["thr" + t], T["sg" + t], T["acc" + t], T["pl" + t], T["plf" + t]
+        lone, thr, sg, acc, pl, plf = T["lone" + t], T["thr" + t], T["sg" + t], T["acc" + t], T["pl" + t], T["plf" + t]
         cmp_, sm, od, later = T["cmp" + t], T["sum" + t], T["ord" + t], T["later" + t]
         hs = 1 - hf
         ae, al, pos = PAR["ae" + t], PAR["al" + t], PAR["pos" + t]
         lo = KH - (al if hf else ae)
         hi = lo + ae + al
+        a1, z1, a2, z2 = H * hf, H * hf + H, H * hs, H * hs + H
         last = {}
 
         def nm(*a):
             return t + "".join(str(x) + "." for x in a)
 
-        def scores(h, a, b):
-            return row[:, 16 + H * h + a:16 + H * h + b]
-
         def of_half(h, scalar):
             return [k for k in range(KH * h, KH * h + KH) if (lo <= k < hi) == scalar]
 
         def own(k):
-            c = 16 * (k // KH) + k % KH
-            return thr[:, c:c + 1]
+            return thr[:, 16 * k + 15:16 * k + 16]
+
+        def at(q, x, y, a, b):
+            if (a, b) == (0, C):
+                return T["ps%d" % (3 if q == "v" else 2)][:, x:y], nm("w" + q)
+            bank = (5 if a == a1 else 7) - (q == "a")
+            return T["ps%d" % bank][:, x - a:y - a], nm("p" + q, a // H)
 
         def owns(h):
-            bank = T["ps%d" % (5 if h == hf else 3)]
-            turn(nm("t2", h), trf[:, TW * h + H + 32:TW * h + TW], bank[:, 0:H], nm("pv", h))
-            turn(nm("t1", h), trf[:, TW * h:TW * h + H + 32], row[:, H * h:H * h + H + 32], nm("r", h))
+            row, tok = at("v", H * h, H * h + H, H * h, H * h + H)
+            tt(nm("t1", h), lone[:, H * h:H * h + H], row, T.one[:], ALU.mult, tok, "one")
 
         def thresholds(h):
-            take("v", nm("th", h), thr[:, 16 * h:16 * h + 16], trf[:, TW * h:TW * h + TW], T.tl2[:, 0:1], "tl2", nm("t1", h), nm("t2", h))
+            scan(nm("th", h), thr[:, H * h:H * h + H], T.keep[:], lone[:, H * h:H * h + H], 0.0, ALU.mult, ALU.add, nm("t1", h), "keep")
 
-        def compare(k, a, b, *after):
+        def compare(k, a, b):
             n, c = 16 * k + 16, C * k
             for x, y, how in ((a, min(b, n), ALU.is_lt), (max(a, n), b, ALU.is_le)):
                 if x < y:
-                    last["cm", k] = ts(nm("cm", k, x), cmp_[:, c + x:c + y], row[:, 16 + x:16 + y], own(k), -0.5, how, ALU.add, nm("th", k // KH), *after)
+                    row, tok = at("v", x, y, a, b)
+                    last["cm", k] = ts(nm("cm", k, x), cmp_[:, c + x:c + y], row, own(k), -0.5, how, ALU.add, nm("th", k // KH), tok)
 
         def total(k):
             scan(nm("sum", k), sm[:, H * k:H * k + H], cmp_[:, C * k:C * k + H], cmp_[:, C * k + H:C * k + C],
                  later[:, 16 * k + 15:16 * k + 16], ALU.add, ALU.add, last["cm", k], nm("lt", k // KH))
 
         def same(h):
-            tt(nm("same", h), T["same" + t][:, H * h:H * h + H], thr[:, 16 * h:16 * h + 16].indirect(T.kl[:, 0:KH]), scores(h, 0, H), ALU.is_equal, nm("th", h), "kl")
+            row, tok = at("v", H * h, H * h + H, H * h, H * h + H)
+            tt(nm("same", h), T["same" + t][:, H * h:H * h + H], thr[:, H * h:H * h + H], row, ALU.is_equal, nm("th", h))
 
         def behind(h):
             scan(nm("lt", h), later[:, H * h:H * h + H], T["same" + t][:, H * h:H * h + H], T.mask[:], 0.0, ALU.add, ALU.mult, nm("same", h), "mask")
@@ -298,9 +299,10 @@ def rank_program(g, core, T, topo):
             tt(nm("wa", h), sg[:, SGW * ks[0] + C:SGW * (ks[-1] + 1):SGW], later[:, 16 * ks[0] + 15:16 * ks[-1] + 16:16], T.k15[:, ks[0]:ks[-1] + 1],
                ALU.subtract, nm("lt", h), "k15")
 
-        def sign(k, a, b, *after):
+        def sign(k, a, b):
             c = SGW * k
-            last["sn", k] = act(nm("sn", k, a, b), sg[:, c + a:c + b], row[:, 16 + a:16 + b], ACT.Sign, nm("th", k // KH), *after, bias=own(k), scale=-1.0)
+            row, tok = at("a", a, b, a, b)
+            last["sn", k] = act(nm("sn", k, a, b), sg[:, c + a:c + b], row, ACT.Sign, nm("th", k // KH), tok, bias=own(k), scale=-1.0)
 
         def smaller(k):
             v = sg[:, SGW * k:SGW * k + 16 * k + 16]
@@ -327,28 +329,18 @@ def rank_program(g, core, T, topo):
         def spread(a, b, *after):
             return op("v", nm("sc", a), lambda: V.tensor_copy(od[:, 16:C + 16].indirect(pl[:, a:b]), T.num[:, 16 * a:16 * b]), "num", *after)
 
-        a1, z1, a2, z2 = H * hf, H * hf + H, H * hs, H * hs + H
-        r = nm("r", hs)
-
-        act(nm("r", hf), scores(hf, 0, H), T.ps4[:, 0:H], ACT.Copy, nm("pa", hf), "padA" + t, "padB" + t, "padC" + t)
         ka, kb = of_half(hf, True), of_half(hs, True)
         e0 = PAR["e0" + t]
         for k in ka[:e0]:
             sign(k, a1, z1)
-        if t == "2":
-            for k in ka[:PAR["ea"]]:
-                (larger if hf else smaller)(k)
-            arrive_a()
-            for k in ka[PAR["ea"]:e0]:
-                (larger if hf else smaller)(k)
-        act(r, scores(hs, 0, H), T.ps2[:, 0:H], ACT.Copy, nm("pa", hs), nm("t1", hf))
-        if t == "1":
-            for k in ka[:e0]:
-                smaller(k)
+        for i, k in enumerate(ka[:e0]):
+            if i == PAR["ea"]:
+                arrive_a()
+            (larger if hf else smaller)(k)
         for k in ka[:e0]:
-            sign(k, a2, z2, r)
+            sign(k, a2, z2)
         whole = ka[e0:] + (kb if hf else kb[::-1])
-        sign(whole[0], 0, C, r)
+        sign(whole[0], 0, C)
         for k in ka[:e0]:
             (smaller if hf else larger)(k)
         for i, k in enumerate(whole):
@@ -375,7 +367,7 @@ def rank_program(g, core, T, topo):
         if pos >= v0 - 2:
             arrive_v()
         owns(hs)
-        compare(ke[0], a2, z2, r)
+        compare(ke[0], a2, z2)
         thresholds(hs)
         compare(ke[1], a2, z2)
         same(hs)
@@ -414,8 +406,11 @@ def rank_program(g, core, T, topo):
             dma("s", "st", "so%s%d" % (t, k), out[k:k + 1, :], T["of" + t][16 * k:16 * k + 1, :], "of" + t)
 
     def score_mm(t, w, x, h, first, *after):
-        mm(t + "pa.%d." % h, 4 if first else 2, w, 0, x, H * h, H * h + H, *after)
-        mm(t + "pv.%d." % h, 5 if first else 3, w, 0, x, H * h, H * h + H)
+        mm(t + "pv.%d." % h, 5 if first else 7, w, 0, x, H * h, H * h + H, *after)
+        mm(t + "pa.%d." % h, 4 if first else 6, w, 0, x, H * h, H * h + H)
+        if not first:
+            mm(t + "wa.", 2, w, 0, x, 0, C)
+            mm(t + "wv.", 3, w, 0, x, 0, C)
 
     mine, pairs = plan_of(rank, T, topo)
     off = topo.engines(core, T.cores[mine[0]])
@@ -472,7 +467,7 @@ def rank_program(g, core, T, topo):
                 turn("u1%d" % h, T.trb1[:, TW * h:TW * h + H + 32], T.ord1[:, H * h:H * h + H + 32], ord1)
                 turn("u2%d" % h, T.trb1[:, TW * h + H + 32:TW * h + TW], T.ord1[:, 16 + H * h:16 + H * h + H])
             elif c[0] in "lL":
-                ts("l0%d" % h, T.l41[:, 16 * h:16 * h + 16], T.trb1[:, TW * h:TW * h + TW].indirect(T.tl2[:, 0:1]), 4.0, 4.0 * H, ALU.mult, ALU.add, "u2%d" % h)
+                ts("l0%d" % h, T.l41[:, 16 * h:16 * h + 16], T.trb1[:, TW * h:TW * h + TW].indirect(T.tl2[:, 0:1]), 4.0, 4.0 * H, ALU.mult, ALU.add, "u2%d" % h, "tl2")
             elif c[0] in "mM":
                 ts("l1%d" % h, T.l41[:, 32 + 16 * h:48 + 16 * h], T.l41[:, 16 * h:16 * h + 16], 2.0, None, ALU.add, None, "l0%d" % h)
             elif c == "o":

from concourse.bass import DstId, RemoteDMATransfer
from concourse.mybir import dt, AluOpType as ALU, ActivationFunctionType as ACT

N, C, S = 8, 384, 48
H = C // 2
KB = C // 16
KH = KB // 2
TW = 2 * H + 32
SGW = C + 8
PAR = {"ae1": 5, "al1": 6, "ae2": 5, "al2": 6, "e01": 2, "e02": 5, "ea": 2, "v01": 3, "v02": 7, "pos1": -1, "pos2": 3, "la2": 2,
       "sa1": 2, "sa2": 2, "nl1": 2, "nl2": 2,
       "fa": "x1w x3w y1w y3w y2a o", "fv": "u l U m x0w L x2w M q0 y0w y2b q1",
       "sa": "f1w f3w x1w x0w x3w y1w y0w y3a", "sv": "f0w s1 s0 f2w s3 s2 x2w q0 y2w y3b q1",
       "adds": "l0 l1 e0 e1 l2 e2 l3 e3", "ha": "00 10 20 01 11 y0 S2 S3 Y1", "hv": "30 q0 31 21 q1 y1", "hs": "C0 Y0 C1 S0 S1"}
SPAN = {"w": (0, H), "a": (0, H // 2), "b": (H // 2, H)}

CODE, PLANE, BF, F32, U16, I32 = "float8_e4m3fn_x4", "uint8", "bfloat16", "float32", "uint16", "int32"
SCRATCH = {}


def _sb(name, cols, dtype):
    SCRATCH[name] = ("sbuf", [128, cols], dtype)


for _n, _c in (("xs", 4 * C), ("us", 512), ("vs", 512), ("ms", 512), ("ft", 4 * C), ("ht", 4 * C), ("hs", 4 * C), ("ss", 4 * C),
               ("tt", 4 * C), ("zs", 4 * C), ("zt", 4 * C), ("et", 2048), ("eo", 2048), ("mi", H), ("mask", H), ("one", H), ("keep", H),
               ("num", C), ("half", C), ("xs1", 4 * C + 16), ("ht1", 4 * C + 16)):
    _sb(_n, _c, BF)
for _n, _c in (("xq", C), ("uq", 128), ("up", 128), ("vq", 128), ("vp", 128), ("mq", 128), ("wq", 512), ("eq4", 512), ("fq", C),
               ("aq", C), ("hq", C), ("tq", C), ("bq", C), ("zq", C), ("r1", 2 * S), ("r2", 2 * S)):
    _sb(_n + "c", _c, CODE)
    _sb(_n + "s", _c, PLANE)
for _t in "12":
    for _n, _c, _d in (("lone", C, F32), ("thr", C, F32), ("same", C, BF), ("later", C, BF),
                       ("cmp", KB * C, BF), ("sum", KB * H, BF), ("sg", KB * SGW, F32), ("acc", 2 * KB, F32), ("plf", KB, F32), ("pl", KB, U16),
                       ("ord", C + 32, BF), ("trb", 2 * TW, BF), ("l4", 64, U16), ("of", C, F32)):
        _sb(_n + _t, _c, _d)
for _n, _c, _d in (("i8", 8, I32), ("pick", 8, U16), ("pi", 1, I32), ("b0", 1, I32), ("b1", 1, I32),
                   ("b2", 1, I32), ("sf", 1, F32), ("e1", 1, F32), ("e2", 1, F32), ("c2", 4, F32), ("k2", 2, F32), ("tl", 2, U16),
                   ("k15", KB, F32), ("e3", 1, F32), ("k3", 2, F32), ("tl2", 2, U16), ("mine", 4, U16), ("y0", H, F32), ("y1", H, F32)):
    _sb(_n, _c, _d)
for _b in range(8):
    SCRATCH["ps%d" % _b] = ("psum", [128, 512], F32)

SEMAPHORES = ["cv", "ca", "ct", "cp", "lu", "lxa", "lxb", "lv", "lm", "lw", "lx", "lh", "far1", "far2", "near1", "near2",
              "hc1", "hs1", "hc2", "hs2", "sent", "st", "sta"]
STAGES = (("fq", "r1", "aq", "1"), ("tq", "r2", "bq", "2"))


def bits(engines):
    m = 0
    for e in engines:
        m |= 1 << e
    return m


def words(view):
    return view.bitcast(dt.uint8)


def plan_of(r, T, topo):
    me = T.cores[r]
    free = [c for c in topo.cores_of(me) if T.rank_of(c) is None and topo.die(c) != topo.die(me)]
    hf = r // (N // 2)
    pairs = []
    for i in range(2):
        m = 2 * (1 - hf) + (r // 2 + i) % 2
        ds = [2 * m, 2 * m + 1]
        c = [c for c in free if all(topo.may_write(c, T.cores[d]) for d in ds)][0]
        free.remove(c)
        pairs.append((c, ds))
    mine = [d for d in range(hf * N // 2, (hf + 1) * N // 2) if d != r]
    mine.sort(key=lambda d: (not topo.mates(me, T.cores[d]), topo.same_plane(me, T.cores[d])))
    return mine, pairs


def transfer(topo, src_core, dst_core, engines, sem, src, dst):
    rid, pid = topo.addr(dst_core, src_core)
    return RemoteDMATransfer(dst_ids=[DstId(rid=rid, pnc=pid)], dma_engine_mask=bits(engines), remote_sem=sem, src=src, dst=dst)


def cols(T, name, kind, a, b):
    v = T[name + kind][:, a:b]
    return words(v) if kind == "c" else v


def relay_engines(t, kind, i, eng, off):
    if t == "2" and kind == "c":
        return eng[8 * i:8 * i + 8]
    return [e for e in eng if e not in off][4 * i:4 * i + 4]


def helper_program(g, core, T, topo):
    for r in range(N):
        mine, pairs = plan_of(r, T, topo)
        for j, (c, ds) in enumerate(pairs):
            if c != core:
                continue
            sent = 0
            me = T.cores[r]
            for src, rel, dst, t in STAGES:
                for kind in "cs":
                    g.wait_ge(T.sem["h" + kind + t], len(relay_engines(t, kind, j, topo.engines(me, c), topo.engines(me, T.cores[mine[0]]))))
                    ts = []
                    for i, d in enumerate(ds):
                        ts.append(transfer(topo, core, T.cores[d], topo.engines(core, T.cores[d])[4 * i:4 * i + 4], T.sem["far" + t],
                                           cols(T, rel, kind, S * i, S * i + S), cols(T, dst, kind, S * r, S * r + S)))
                        sent += 4
                    g.remote_dma_fused(ts, local_sem=T.sem.sent)
            g.wait_ge(T.sem.sent, sent)


def rank_program(g, core, T, topo):
    rank = T.rank_of(core)
    if rank is None:
        helper_program(g, core, T, topo)
        return
    Q = {"v": g.vector, "a": g.scalar, "t": g.tensor, "p": g, "s": g.sync}
    V, A, PE = g.vector, g.scalar, g.tensor
    cnt = {"sent": 0}
    seen = {q: {} for q in Q}
    todo = {q: [] for q in Q}
    done = {"near1": ("near1", 16), "near2": ("near2", 16), "far1": ("far1", 32), "far2": ("far2", 32)}

    def wait(q, toks):
        need = {}
        for s, n in toks:
            need[s] = max(need.get(s, 0), n)
        for s in need:
            if seen[q].get(s, 0) < need[s]:
                Q[q].wait_ge(T.sem[s], need[s])
                seen[q][s] = need[s]

    def issue():
        while any(todo.values()):
            moved = False
            for q in Q:
                while todo[q] and all(a in done for a in todo[q][0][4]):
                    name, s, step, call, after = todo[q].pop(0)
                    wait(q, [done[a] for a in after])
                    if s is None:
                        call()
                    else:
                        cnt[s] = cnt.get(s, 0) + step
                        call().then_inc(T.sem[s], step)
                        done[name] = (s, cnt[s])
                    moved = True
            assert moved

    def op(q, name, call, *after):
        todo[q].append((name, "c" + q, 1, call, after))
        return name

    def dma(q, s, name, out, in_, *after):
        todo[q].append((name, s, 16, lambda: Q[q].dma_start(out, in_), after))
        return name

    def quant(name, q, tile, a, b, *after):
        return op("v", name, lambda: V.quantize_mx(T[q + "c"][:, a:b], T[q + "s"][:, a:b], tile[:, 4 * a:4 * b]), *after)

    def mm(name, bank, w, a, x, c, d, *after):
        return op("t", name, lambda: PE.matmul_mx(T["ps%d" % bank][:, 0:d - c], T[w + "c"][:, a:a + 128], T[w + "s"][:, a:a + 128],
                                                  T[x + "c"][:, c:d], T[x + "s"][:, c:d], True, True), *after)

    def ts(name, out, in0, s1, s2, o0, o1, *after):
        if o1 is None:
            return op("v", name, lambda: V.tensor_scalar(out, in0, s1, None, o0), *after)
        return op("v", name, lambda: V.tensor_scalar(out, in0, s1, s2, o0, o1), *after)

    def tt(name, out, in0, in1, how, *after):
        return op("v", name, lambda: V.tensor_tensor(out, in0, in1, how), *after)

    def scan(name, out, d0, d1, first, o0, o1, *after):
        return op("v", name, lambda: V.tensor_tensor_scan(out, d0, d1, first, o0, o1), *after)

    def copy(name, out, in_, *after):
        return op("v", name, lambda: V.tensor_copy(out, in_), *after)

    def turn(name, out, in_, *after):
        return op("v", name, lambda: V.transpose(out, in_), *after)

    def fill(name, out, value, *after):
        return op("v", name, lambda: V.memset(out, value), *after)

    def act(name, out, in_, func, *after, **kw):
        return op("a", name, lambda: A.activation(out, in_, func, **kw), *after)

    def take(q, name, out, win, off, *after):
        if q == "v":
            return copy(name, out, win.indirect(off), *after)
        return act(name, out, win.indirect(off), ACT.Copy, *after)

    def iota(name, pattern, base, cm, whole):
        if whole:
            return op("p", name, lambda: g.iota(T[name][:], pattern, base, cm))
        return op("p", name, lambda: g.iota(T[name][:], pattern, base, cm, allow_small_or_imprecise_dtypes=True))

    hl = rank // (N // 2)
    he = 1 - hl

    dma("a", "lu", "lu", T.us[:], T.u[:])
    dma("s", "lxa", "lxa", T.xs[:, 0:4 * H], T.x[:, 0:4 * H])
    dma("s", "lxb", "lxb", T.xs[:, 4 * H:4 * C], T.x[:, 4 * H:4 * C])
    dma("s", "lx", "lx1", T.xs1[:, 15:15 + 4 * C], T.x[:], "lu", "lxa", "lxb")
    dma("s", "lw", "lw0", words(T.wqc[:]), T.wc[:])
    dma("s", "lw", "lw", T.wqs[:], T.ws[:])
    dma("s", "lv", "lv", T.vs[:], T.v[:])
    dma("s", "lm", "lm", T.ms[:], T.m[:])

    iota("i8", [[16, 8]], 0, 0, True)
    iota("pi", [[1, 1]], 0, 1, True)
    iota("mi", [[0, KH], [1, 16]], 0, 0, False)
    iota("c2", [[16, 4]], 0, 0, False)
    iota("k15", [[16, KB]], 15, 0, False)
    iota("num", [[1, C]], -H, 0, False)
    op("p", "half", lambda: g.affine_select(T.half[:], T.num[:], [[0, C]], ALU.is_gt, 0.5, 0, 0), "num")
    iota("eo", [[0, 2048]], 1, 0, False)
    op("p", "et", lambda: g.affine_select(T.et[:], T.eo[:], [[-1, 4], [1, 512]], ALU.is_equal, 0.0, 0, -4), "eo")

    def margins(t):
        fill("padD" + t, T["ord" + t][:, 0:16], 0.0)
        fill("padE" + t, T["ord" + t][:, C + 16:C + 32], 0.0)

    margins("1")
    copy("pick", T.pick[:], T.i8[:], "i8")
    ts("b0", T.b0[:], T.pi[:], 15, None, ALU.bitwise_and, None, "pi")
    ts("b1", T.b1[:], T.pi[:], 1, None, ALU.bitwise_and, None)
    ts("b2", T.b2[:], T.pi[:], 4, 1, ALU.logical_shift_right, ALU.bitwise_and)
    copy("sf", T.sf[:], T.b0[:], "b0")
    tt("e1", T.e1[:], T.b1[:], T.b2[:], ALU.is_equal, "b1", "b2")
    ts("keep", T.keep[:], T.mi[:], 1.0, None, ALU.min, None, "mi")
    ts("one", T.one[:], T.mi[:], T.sf[:], None, ALU.is_equal, None, "sf")
    ts("mask", T.mask[:], T.mi[:], T.sf[:], None, ALU.is_gt, None)
    ts("k2", T.k2[:], T.c2[:, 0:2], T.sf[:], float(KB - 1), ALU.add, ALU.min, "c2")
    ts("k3", T.k3[:], T.c2[:, 0:2], T.sf[:], float(KH - 1), ALU.add, ALU.min)
    ts("e2", T.e2[:], T.e1[:], float(C + 16), 16.0, ALU.mult, ALU.add, "e1")
    ts("e3", T.e3[:], T.e1[:], float(H + 16), 16.0, ALU.mult, ALU.add)
    ts("mine", T.mine[:], T.c2[:], T.sf[:], float(S * rank - H * hl), ALU.add, ALU.add)
    ts("tl", T.tl[:], T.k2[:], 16.0, T.e2[:], ALU.mult, ALU.add, "k2", "e2")
    ts("tl2", T.tl2[:], T.k3[:], 16.0, T.e3[:], ALU.mult, ALU.add, "k3", "e3")

    def sixteen(q, p, tok):
        copy(p + "c", T[p + "c"][:].bitcast(dt.uint32), T[q + "c"][:].bitcast(dt.uint32).indirect(T.pick[:]), tok, "pick")
        take("a", p + "s", T[p + "s"][:], T[q + "s"][:], T.pick[:], tok, "pick")
        return p + "c", p + "s"

    def sorter(t, hf, arrive_v, arrive_a):
        lone, thr, sg, acc, pl, plf = T["lone" + t], T["thr" + t], T["sg" + t], T["acc" + t], T["pl" + t], T["plf" + t]
        cmp_, sm, od, later = T["cmp" + t], T["sum" + t], T["ord" + t], T["later" + t]
        hs = 1 - hf
        ae, al, pos = PAR["ae" + t], PAR["al" + t], PAR["pos" + t]
        lo = KH - (al if hf else ae)
        hi = lo + ae + al
        a1, z1, a2, z2 = H * hf, H * hf + H, H * hs, H * hs + H
        last = {}

        def nm(*a):
            return t + "".join(str(x) + "." for x in a)

        def of_half(h, scalar):
            return [k for k in range(KH * h, KH * h + KH) if (lo <= k < hi) == scalar]

        def own(k):
            return thr[:, 16 * k + 15:16 * k + 16]

        def at(q, x, y, a, b):
            if (a, b) == (0, C):
                return T["ps%d" % (3 if q == "v" else 2)][:, x:y], nm("w" + q)
            bank = (5 if a == a1 else 7) - (q == "a")
            return T["ps%d" % bank][:, x - a:y - a], nm("p" + q, a // H)

        def owns(h):
            row, tok = at("v", H * h, H * h + H, H * h, H * h + H)
            tt(nm("t1", h), lone[:, H * h:H * h + H], row, T.one[:], ALU.mult, tok, "one")

        def thresholds(h):
            scan(nm("th", h), thr[:, H * h:H * h + H], T.keep[:], lone[:, H * h:H * h + H], 0.0, ALU.mult, ALU.add, nm("t1", h), "keep")

        def compare(k, a, b):
            n, c = 16 * k + 16, C * k
            for x, y, how in ((a, min(b, n), ALU.is_lt), (max(a, n), b, ALU.is_le)):
                if x < y:
                    row, tok = at("v", x, y, a, b)
                    last["cm", k] = ts(nm("cm", k, x), cmp_[:, c + x:c + y], row, own(k), -0.5, how, ALU.add, nm("th", k // KH), tok)

        def total(k):
            scan(nm("sum", k), sm[:, H * k:H * k + H], cmp_[:, C * k:C * k + H], cmp_[:, C * k + H:C * k + C],
                 later[:, 16 * k + 15:16 * k + 16], ALU.add, ALU.add, last["cm", k], nm("lt", k // KH))

        def same(h):
            row, tok = at("v", H * h, H * h + H, H * h, H * h + H)
            tt(nm("same", h), T["same" + t][:, H * h:H * h + H], thr[:, H * h:H * h + H], row, ALU.is_equal, nm("th", h))

        def behind(h):
            scan(nm("lt", h), later[:, H * h:H * h + H], T["same" + t][:, H * h:H * h + H], T.mask[:], 0.0, ALU.add, ALU.mult, nm("same", h), "mask")

        def for_scalar(h):
            ks = of_half(h, True)
            tt(nm("wa", h), sg[:, SGW * ks[0] + C:SGW * (ks[-1] + 1):SGW], later[:, 16 * ks[0] + 15:16 * ks[-1] + 16:16], T.k15[:, ks[0]:ks[-1] + 1],
               ALU.subtract, nm("lt", h), "k15")

        def sign(k, a, b):
            c = SGW * k
            row, tok = at("a", a, b, a, b)
            last["sn", k] = act(nm("sn", k, a, b), sg[:, c + a:c + b], row, ACT.Sign, nm("th", k // KH), tok, bias=own(k), scale=-1.0)

        def smaller(k):
            v = sg[:, SGW * k:SGW * k + 16 * k + 16]
            last["done", k] = act(nm("sm", k), v, v, ACT.Relu, last["sn", k], accum_out=acc[:, k:k + 1])

        def larger(k):
            v = sg[:, SGW * k + 16 * k + 16:SGW * k + C + 1]
            last["done", k] = act(nm("lg", k), v, v, ACT.Relu, last["sn", k], nm("wa", k // KH), scale=-1.0, accum_out=acc[:, KB + k:KB + k + 1])

        def places_v(ks):
            return ts(nm("p0", ks[0]), pl[:, ks[0]:ks[-1] + 1], sm[:, H * ks[0] + H - 1:H * ks[-1] + H:H], -1.0, H - 1.0, ALU.mult, ALU.add, nm("sum", ks[-1]))

        def diff_a(ks):
            a, b = ks[0], ks[-1] + 1
            return tt(nm("d", a), plf[:, a:b], acc[:, KB + a:KB + b], acc[:, a:b], ALU.subtract, *[last["done", k] for k in ks])

        def places_a(ks):
            a, b = ks[0], ks[-1] + 1
            return copy(nm("p1", a), pl[:, a:b], plf[:, a:b], nm("d", a))

        def place_a(k):
            return ts(nm("p2", k), pl[:, k:k + 1], acc[:, KB + k:KB + k + 1], acc[:, k:k + 1], None, ALU.subtract, None, last["done", k])

        def spread(a, b, *after):
            return op("v", nm("sc", a), lambda: V.tensor_copy(od[:, 16:C + 16].indirect(pl[:, a:b]), T.num[:, 16 * a:16 * b]), "num", *after)

        ka, kb = of_half(hf, True), of_half(hs, True)
        e0 = PAR["e0" + t]
        for k in ka[:e0]:
            sign(k, a1, z1)
        for i, k in enumerate(ka[:e0]):
            if i == PAR["ea"]:
                arrive_a()
            (larger if hf else smaller)(k)
        for k in ka[:e0]:
            sign(k, a2, z2)
        whole = ka[e0:] + (kb if hf else kb[::-1])
        sign(whole[0], 0, C)
        for k in ka[:e0]:
            (smaller if hf else larger)(k)
        for i, k in enumerate(whole):
            if i + 1 < len(whole):
                sign(whole[i + 1], 0, C)
            smaller(k)
            larger(k)

        ke, kv = of_half(hf, False), of_half(hs, False)
        owns(hf)
        thresholds(hf)
        if pos < 0:
            arrive_v()
        same(hf)
        compare(ke[0], a1, z1)
        behind(hf)
        compare(ke[1], a1, z1)
        for_scalar(hf)
        v0 = PAR["v0" + t]
        for i, k in enumerate(ke[2:v0]):
            if i == pos:
                arrive_v()
            compare(k, a1, z1)
        if pos >= v0 - 2:
            arrive_v()
        owns(hs)
        compare(ke[0], a2, z2)
        thresholds(hs)
        compare(ke[1], a2, z2)
        same(hs)
        total(ke[0])
        behind(hs)
        total(ke[1])
        for_scalar(hs)
        prev = None
        for k in ke[2:] + kv:
            if k in ke[:v0]:
                compare(k, a2, z2)
            else:
                compare(k, 0, C)
            if prev is not None:
                total(prev)
            prev = k
            if k == kv[PAR["sa" + t]]:
                diff_a(ka)
                p0 = places_v(ke)
                p1 = places_a(ka)
        s0 = spread(KH * hf, KH * hf + KH, p0, p1, "padD" + t, "padE" + t)
        total(prev)
        nl = PAR["nl" + t]
        tail = kb[-nl:] if hf else kb[:nl]
        head = [k for k in kb if k not in tail]
        diff_a(head)
        p0 = places_v(kv)
        p1 = places_a(head)
        rest = sorted(head + kv)
        s1 = spread(rest[0], rest[-1] + 1, s0, p0, p1)
        return spread(tail[0], tail[-1] + 1, s1, *[place_a(k) for k in whole[-nl:]])

    def write_order(t, out, tok):
        act("of" + t, T["of" + t][:], T["ord" + t][:, 16:C + 16], ACT.Identity, tok, bias=float(H))
        for k in range(8):
            dma("s", "st", "so%s%d" % (t, k), out[k:k + 1, :], T["of" + t][16 * k:16 * k + 1, :], "of" + t)

    def score_mm(t, w, x, h, first, *after):
        mm(t + "pv.%d." % h, 5 if first else 7, w, 0, x, H * h, H * h + H, *after)
        mm(t + "pa.%d." % h, 4 if first else 6, w, 0, x, H * h, H * h + H)
        if not first:
            mm(t + "wa.", 2, w, 0, x, 0, C)
            mm(t + "wv.", 3, w, 0, x, 0, C)

    mine, pairs = plan_of(rank, T, topo)
    off = topo.engines(core, T.cores[mine[0]])

    def remote(name, tr, *after):
        todo["p"].append((name, None, 0, lambda: g.remote_dma_fused(tr, local_sem=T.sem.sent), after))

    def far(stage, tok):
        src, rel, dst, t = STAGES[stage]
        for kind in "cs":
            tr = []
            for i, (c, ds) in enumerate(pairs):
                eng = relay_engines(t, kind, i, topo.engines(core, c), off)
                tr.append(transfer(topo, core, c, eng, T.sem["h" + kind + t],
                                   cols(T, src, kind, S * ds[0], S * ds[0] + 2 * S), cols(T, rel, kind, 0, 2 * S)))
                cnt["sent"] += len(eng)
            remote("rel" + kind + t, tr, tok)

    def near(stage, tok):
        src, rel, dst, t = STAGES[stage]
        deal = {"c": (off[0:4], off[4:6], off[6:8]), "s": (off[0:2], off[2:4], off[4:8])}
        for kind in "cs":
            tr = []
            for d, eng in zip(mine, deal[kind]):
                tr.append(transfer(topo, core, T.cores[d], eng, T.sem["near" + t],
                                   cols(T, src, kind, S * d, S * d + S), cols(T, dst, kind, S * rank, S * rank + S)))
            cnt["sent"] += 8
            remote("near" + kind + t, tr, tok)

    def keep(stage, tok):
        src, rel, dst, t = STAGES[stage]
        a, b = S * rank, S * rank + S
        copy("ownc" + t, T[dst + "c"][:, a:b].bitcast(dt.uint32), T[src + "c"][:, H * hl:H * hl + H].bitcast(dt.uint32).indirect(T.mine[:, 0:3]), tok, "mine")
        return take("v", "owns" + t, T[dst + "s"][:, a:b], T[src + "s"][:, H * hl:H * hl + H], T.mine[:, 0:3], tok)

    def moved(name, b):
        return T[name + "1"][:, 16:15 + 4 * C] if b % 2 else T[name][:]

    def send(stage, name, tile, h, mark, key, steps):
        got = [mark + "%s.%d" % (e[1], H * h + SPAN[e[2]][0]) for e in steps.split() if e[0] == key]
        (near if h == hl else far)(stage, quant(name + str(h), STAGES[stage][0], tile, H * h, H * h + H, *got))

    quant("qu", "uq", T.us, 0, 128, "lu")
    up = sixteen("uq", "up", "qu")
    quant("qx0", "xq", T.xs, 0, H, "lxa")
    score_mm("1", "up", "xq", 0, True, "qx0", *up)
    score_mm("1", "up", "xq", 1, False, "qx1")
    ord1 = sorter("1", 0, lambda: quant("qx1", "xq", T.xs, H, C, "lxb"), lambda: None)

    for q in "av":
        for c in PAR["f" + q].split():
            h = he if c[0] in "yULM" or c == "q1" else hl
            if c[0] in "uU":
                turn("u1%d" % h, T.trb1[:, TW * h:TW * h + H + 32], T.ord1[:, H * h:H * h + H + 32], ord1)
                turn("u2%d" % h, T.trb1[:, TW * h + H + 32:TW * h + TW], T.ord1[:, 16 + H * h:16 + H * h + H])
            elif c[0] in "lL":
                ts("l0%d" % h, T.l41[:, 16 * h:16 * h + 16], T.trb1[:, TW * h:TW * h + TW].indirect(T.tl2[:, 0:1]), 4.0, 4.0 * H, ALU.mult, ALU.add, "u2%d" % h, "tl2")
            elif c[0] in "mM":
                ts("l1%d" % h, T.l41[:, 32 + 16 * h:48 + 16 * h], T.l41[:, 16 * h:16 * h + 16], 2.0, None, ALU.add, None, "l0%d" % h)
            elif c == "o":
                write_order("1", T.oa, ord1)
            elif c[0] == "q":
                send(0, "qf", T.ft, h, "f", "xy"[int(c[1])], PAR["fa"] + " " + PAR["fv"])
            else:
                b, (x, y) = int(c[1]), SPAN[c[2]]
                a = 32 * (b // 2) + 16 * h
                take(q, "f%d.%d" % (b, H * h + x), T.ft[:, 4 * (H * h + x) + b:4 * (H * h + y):4], moved("xs", b), T.l41[:, a + x // 16:a + y // 16],
                     "l%d%d" % (b // 2, h), "lxa", "lxb", "lx1")
    own1 = keep(0, "qf%d" % hl)

    quant("qv", "vq", T.vs, 0, 128, "lv")
    margins("2")
    vp = sixteen("vq", "vp", "qv")

    def layer_mm(h, banks, *after):
        for b in (1, 0, 3, 2):
            mm("r%d%d" % (b, h), banks[b], "wq", 128 * b, "aq", H * h, H * h + H, "lw", *after)

    def layer(q, h, banks, bs):
        for b in bs:
            out, ps = T.ht[:, 4 * H * h + b:4 * H * (h + 1):4], T["ps%d" % banks[b]][:, 0:H]
            if q == "a":
                act("h%d%d" % (b, h), out, ps, ACT.Copy, "r%d%d" % (b, h), scale=0.00390625)
            else:
                ts("h%d%d" % (b, h), out, ps, 0.00390625, None, ALU.mult, None, "r%d%d" % (b, h))

    def quant_h(h):
        quant("qh%d" % h, "hq", T.ht, H * h, H * h + H, *["h%d%d" % (b, h) for b in range(4)])

    layer_mm(hl, (0, 1, 2, 3), own1, "near1", "qf0", "qf1")
    layer("a", hl, (0, 1, 2, 3), (1, 3))
    layer("v", hl, (0, 1, 2, 3), (0, 2))
    quant_h(hl)
    score_mm("2", "vp", "hq", hl, True, "qh%d" % hl, *vp)
    layer_mm(he, (6, 7, 0, 1), "far1")
    score_mm("2", "vp", "hq", he, False, "qh%d" % he)
    dma("s", "lh", "lh1", T.ht1[:, 15:15 + 4 * C], T.ht[:], "qh0", "qh1")
    on_a = (1, 0, 3, 2)[:PAR["la2"]]

    def arrive_v():
        layer("v", he, (6, 7, 0, 1), [b for b in (1, 0, 3, 2) if b not in on_a])
        quant_h(he)

    ord2 = sorter("2", hl, arrive_v, lambda: layer("a", he, (6, 7, 0, 1), on_a))
    turn("w1", T.trb2[:, 0:C + 32], T.ord2[:], ord2)
    turn("w2", T.trb2[:, C + 32:2 * C + 32], T.ord2[:, 16:C + 16])
    ts("m0", T.l42[:, 0:32], T.trb2[:, 0:2 * C + 32].indirect(T.tl[:]), 4.0, 4.0 * H, ALU.mult, ALU.add, "w2", "tl")
    write_order("2", T.ob, ord2)

    def back(q, name, out, src, pl, b, a, z, *after):
        return take(q, name + "%d.%d" % (b, a), out[:, 4 * a + b:4 * z:4], src[:, C * b:C * b + C], pl[:, a // 16:z // 16], *after)

    ts("m1", T.l42[:, 32:32 + KB], T.l42[:, 0:KB], 2.0, None, ALU.add, None, "m0")
    for q in "av":
        for c in PAR["s" + q].split():
            b = int(c[1])
            h = hl if c[0] == "y" or c == "q1" else he
            if c[0] == "f":
                take(q, "fw%d" % b, T.hs[:, C * b:C * b + C], moved("ht", b), T.l42[:, 32 * (b // 2):32 * (b // 2) + KB], "m%d" % (b // 2), "lh1")
            elif c[0] == "s":
                scan("s%d" % b, T.ss[:, C * b:C * b + C], T.half[:], T.hs[:, C * b:C * b + C], 0.0, ALU.mult, ALU.max, "fw%d" % b, "half")
            elif c[0] == "q":
                send(1, "qt", T.tt, h, "t", "xy"[b], PAR["sa"] + " " + PAR["sv"])
            else:
                x, y = SPAN[c[2]]
                back(q, "t", T.tt, T.ss, T.pl2, b, H * h + x, H * h + y, "s%d" % b)
    own2 = keep(1, "qt%d" % hl)

    quant("qe", "eq4", T.et, 0, 512, "et")
    quant("qm", "mq", T.ms, 0, 128, "lm")

    def add(b, h):
        bank = (4 if h == hl else 0) + b
        mm("d%d%d" % (b, h), bank, "eq4", 128 * b, "bq", H * h, H * h + H, "qe", "qt0", "qt1", *((own2, "near2") if h == hl else ("far2",)))
        tt("z%d%d" % (b, h), T.zs[:, C * b + H * h:C * b + H * h + H], T["ps%d" % bank][:, 0:H], T.ft[:, 4 * H * h + b:4 * H * (h + 1):4], ALU.add, "d%d%d" % (b, h))

    def step(q, c):
        i = int(c[1])
        a, z = H * i, H * i + H
        st = "st" if q == "s" else "sta"
        if c[0] == "q":
            quant("qz%d" % i, "zq", T.zt, a, z, *["o%d.%d" % (b, a) for b in range(4)])
            mm("y%d" % i, 4 + i, "mq", 0, "zq", a, z, "qz%d" % i, "qm")
        elif c[0] == "y":
            if q == "a":
                act("c%d" % i, T["y%d" % i][:], T["ps%d" % (4 + i)][:, 0:H], ACT.Copy, "y%d" % i)
            else:
                copy("c%d" % i, T["y%d" % i][:], T["ps%d" % (4 + i)][:, 0:H], "y%d" % i)
        elif c[0] == "C":
            dma(q, st, "sc%d" % i, T.oc[:, 4 * a:4 * z], words(T.zqc[:, a:z]), "qz%d" % i)
        elif c[0] == "Y":
            dma(q, st, "sy%d" % i, T.y[:, a:z], T["y%d" % i][:], "c%d" % i)
        elif c[0] == "S":
            dma(q, st, "ss%d" % i, T.osc[4 * i:4 * i + 4, :], T.zqs[32 * i:32 * i + 4, :], "qz1")
        else:
            back(q, "o", T.zt, T.zs, T.pl1, int(c[0]), a, z, "z%s0" % c[0], "z%s1" % c[0])

    for c in PAR["adds"].split():
        add(int(c[1]), hl if c[0] == "l" else he)
    for q in "avs":
        for c in PAR["h" + q].split():
            step(q, c)

    issue()
    wait("p", [(s, cnt[s]) for s in cnt] + [done[s] for s in ("near1", "near2", "far1", "far2")])
